import numpy as np
import ml_dtypes


def mxq(x, axis, fmt="e4m3"):
    dtype, down = {"e4m3": (ml_dtypes.float8_e4m3fn, 7), "e5m2": (ml_dtypes.float8_e5m2, 14)}[fmt]
    v = np.moveaxis(np.asarray(x, np.float32).astype(ml_dtypes.bfloat16).astype(np.float64), axis, -1)
    blocks = v.reshape(v.shape[:-1] + (-1, 32))
    amax = np.abs(blocks).max(-1, keepdims=True)
    byte = np.maximum(np.where(amax > 0, np.frexp(amax)[1] - 1 + 127, 0) - down, 1)
    scale = np.exp2(byte - 127.0)
    codes = (blocks / scale).astype(np.float32).astype(dtype).astype(np.float64)
    return np.moveaxis((codes * scale).reshape(v.shape), -1, axis)


WIDE = False


def mx_kscale(k):
    if not WIDE:
        return np.ones(k)
    levels = np.array([10, -10, 5, -5, 0])
    if k % 512:
        return np.exp2(np.random.permutation(np.resize(levels, k // 32))).repeat(32)
    a = np.empty((k // 512, 16))
    for p in range(k // 512):
        a[p, :8] = np.random.permutation(np.resize(levels, 8))
        for g in range(8):
            far = levels[np.abs(levels - a[p, g]) >= 10]
            a[p, g + 8] = far[np.random.randint(len(far))]
    return np.exp2(a.ravel()).repeat(32)


def f64(x):
    return np.asarray(x).astype(np.float64)


def striped(idx):
    return np.tile(idx.reshape(-1, 16).T, (8, 1)).astype(np.uint16)


def unstriped(offs):
    return offs[:16].T.reshape(-1).astype(np.int64)


def pack_weight(w):
    k, n = w.shape
    w = f64(np.asarray(w, np.float32).astype(ml_dtypes.bfloat16)).reshape(k // 32, 32, n)
    amax = np.abs(w).max(1)
    byte = np.clip(np.where(amax > 0, np.frexp(amax)[1] - 1 + 127 - 7, 1), 1, 254)
    scaled = (w * np.exp2(127.0 - byte)[:, None, :]).reshape(k, n).astype(np.float32)
    words = np.ascontiguousarray(scaled.reshape(k // 512, 128, 4, n).transpose(0, 1, 3, 2)).astype(ml_dtypes.float8_e4m3fn).view(np.uint8)
    return words, np.ascontiguousarray(byte.astype(np.uint8).reshape(k // 512, 16, n))


def unpack_weight(words, scales):
    g, p, n, _ = words.shape
    vals = np.ascontiguousarray(words).view(ml_dtypes.float8_e4m3fn).astype(np.float64) * np.repeat(np.exp2(scales.astype(np.float64) - 127.0), 8, axis=1)[..., None]
    return vals.transpose(0, 1, 3, 2).reshape(g * 512, n)


def relu2(v):
    return np.maximum(v, 0.0) ** 2


K, T, D, S, V, N = 512, 1024, 3, 512, 256, 256


def setup_inputs():
    n = np.random.standard_normal
    s = mx_kscale(K)[:, None]
    words, scales = pack_weight(n((K, N)) / np.sqrt(K) / s)
    return {
        "xT": (n((K, T)) * s).astype(np.float32),
        "w_words": words,
        "w_scales": scales,
        "b": (0.3 * n((N, 1))).astype(np.float32),
        "gate": np.tile(np.random.uniform(0.2, 1.0, (D, 1, V)) / np.sqrt(D), (1, N, 1)).astype(np.float32),
        "offs": striped(np.random.permutation(T)[:S]),
        "pos1": striped(np.random.permutation(S)[:V]),
        "pos2": striped(np.random.permutation(S)[:V]),
        "pos3": striped(np.random.permutation(S)[:V]),
    }


def reference(xT, w_words, w_scales, b, gate, offs, pos1, pos2, pos3):
    w = unpack_weight(w_words, w_scales)
    idx = unstriped(offs)
    xq = mxq(f64(xT)[:, idx], 0, "e4m3")
    y = w.T @ xq
    y = relu2(y + f64(b))
    return sum(f64(gate[d]) * y[:, unstriped(p)] for d, p in enumerate((pos1, pos2, pos3)))

@@ -1,0 +1,137 @@
+from contextlib import ExitStack
+
+import concourse.mybir as mybir
+
+K, T, D, S, V, N = 512, 1024, 3, 512, 256, 256
+FLOPS = 2 * K * S * N
+
+F32 = mybir.dt.float32
+BF16 = mybir.dt.bfloat16
+I32 = mybir.dt.int32
+U16 = mybir.dt.uint16
+U32 = mybir.dt.uint32
+U8 = mybir.dt.uint8
+FP8X4 = mybir.dt.float8_e4m3fn_x4
+ACT = mybir.ActivationFunctionType
+ALU = mybir.AluOpType
+
+P = 128
+G = 16
+
+
+def tile_picked_sub_lin_relu2_sub_e_kernel(tc, xT, w_words, w_scales, b, gate, offs, pos1, pos2, pos3, out):
+    nc = tc.nc
+    with ExitStack() as ctx:
+        lists = ctx.enter_context(tc.tile_pool(name="lists", bufs=1))
+        sb = ctx.enter_context(tc.tile_pool(name="sb", bufs=1))
+        psum = ctx.enter_context(tc.psum_pool(name="psum", bufs=1))
+
+        offs_t = lists.tile([P, S // G], U16, name="offs_t")
+        pos_t = [lists.tile([P, V // G], U16, name=f"pos_t{d}") for d in range(D)]
+        x_rows = xT.rearrange("(p j) t -> p j t", j=4)
+        x = [sb.tile([P, T], F32, name=f"x{j}", align_bytes=64) for j in range(4)]
+        w_codes = sb.tile([P, N], I32, name="w_codes", align_bytes=64)
+        w_plane = sb.tile([P, N], U8, name="w_plane", align_bytes=64)
+        bias = sb.tile([P, 2], F32, name="bias")
+        gates = [sb.tile([P, D, V], F32, name=f"gates{c}", align_bytes=64) for c in range(2)]
+        warm = sb.tile([P, 8], F32, name="warm")
+        warm_out = sb.tile([P, 8], F32, name="warm_out")
+
+        nc.sync.dma_start(x[0][:], x_rows[:, 0, :])
+        nc.sync.dma_start(offs_t[:], offs)
+        for j in range(1, 4):
+            nc.sync.dma_start(x[j][:], x_rows[:, j, :])
+        nc.sync.dma_start(w_codes[:], w_words[0].rearrange("p n t -> p (n t)").bitcast(I32))
+        with nc.allow_non_contiguous_dma(reason="one bias value to a partition"):
+            nc.sync.dma_start(bias[:], b.rearrange("(c p) o -> p (c o)", p=P))
+        for d, pos in enumerate((pos1, pos2, pos3)):
+            nc.sync.dma_start(pos_t[d][:], pos)
+        for c in range(2):
+            nc.sync.dma_start(gates[c][:], gate[:, c * P:(c + 1) * P, :].rearrange("d p v -> p d v"))
+
+        nc.vector.memset(warm[:], 0.0)
+        nc.scalar.activation(warm_out[:], warm[:], ACT.Square)
+        nc.gpsimd.memset(w_plane[:], 0)
+        for q in range(4):
+            nc.gpsimd.dma_start(w_plane[32 * q:32 * q + 4, :].bitcast(I32), w_scales[0, 4 * q:4 * q + 4, :].bitcast(I32))
+
+        def picks(lo, hi):
+            return offs_t[:, lo // G:hi // G]
+
+        spans = [(0, 256), (256, 384), (384, 512)]
+        packed = [sb.tile([P, hi - lo, 4], BF16, name=f"packed{i}", align_bytes=64) for i, (lo, hi) in enumerate(spans)]
+        g01 = sb.tile([P, 2, S], F32, name="g01", align_bytes=64)
+        g23 = sb.tile([P, 2, 384], F32, name="g23", align_bytes=64)
+
+        nc.vector.tensor_copy(g01[:, 0, :], x[0][:].indirect(offs_t[:]))
+        for lo, hi in ((0, 256), (256, 512)):
+            nc.vector.tensor_copy(g01[:, 1, lo:hi], x[1][:].indirect(picks(lo, hi)))
+        for i, (lo, hi) in enumerate(spans):
+            nc.scalar.copy(packed[i][:, :, 0:2], g01[:, :, lo:hi].rearrange("p u n -> p n u"))
+        nc.vector.tensor_copy(g23[:, 0, :], x[2][:].indirect(picks(0, 384)))
+        nc.vector.tensor_copy(packed[2][:, :, 2], x[2][:].indirect(picks(384, 512)))
+        for lo in (0, 128, 256):
+            nc.vector.tensor_copy(g23[:, 1, lo:lo + P], x[3][:].indirect(picks(lo, lo + P)))
+        nc.vector.tensor_copy(packed[2][:, :, 3], x[3][:].indirect(picks(384, 512)))
+        for i, at, lo in ((0, 0, 0), (0, 128, 128), (1, 0, 256)):
+            nc.scalar.copy(packed[i][:, at:at + P, 2:4], g23[:, :, lo:lo + P].rearrange("p u n -> p n u"))
+
+        order = (0, 2, 1)
+        codes, planes, acc = {}, {}, {}
+        for i in order:
+            n = spans[i][1] - spans[i][0]
+            codes[i] = sb.tile([P, n], U32, name=f"codes{i}", align_bytes=64)
+            planes[i] = sb.tile([P, n], U8, name=f"planes{i}", align_bytes=64)
+            nc.vector.quantize_mx(out=codes[i][:].bitcast(FP8X4), scales=planes[i][:], in_=packed[i][:].rearrange("p n j -> p (n j)"))
+        for i, c in ((0, 0), (2, 0), (0, 1), (1, 0), (2, 1), (1, 1)):
+            n = spans[i][1] - spans[i][0]
+            acc[i, c] = psum.tile([P, n], F32, name=f"acc{i}_{c}")
+            nc.tensor.matmul_mx(
+                out=acc[i, c][:],
+                lhsT=w_codes[:, c * P:(c + 1) * P].bitcast(FP8X4),
+                lhsT_scale=w_plane[:, c * P:(c + 1) * P],
+                rhs=codes[i][:].bitcast(FP8X4),
+                rhs_scale=planes[i][:],
+                start=True,
+                stop=True,
+            )
+
+        r = [sb.tile([P, S], F32, name=f"r{c}", align_bytes=64) for c in range(2)]
+        y = [sb.tile([P, S], F32, name=f"y{c}", align_bytes=64) for c in range(2)]
+        lo, hi = spans[0]
+        nc.scalar.activation(r[0][:, lo:hi], acc[0, 0][:], ACT.Relu, bias=bias[:, 0:1])
+        for i in (2, 1):
+            lo, hi = spans[i]
+            nc.vector.tensor_scalar(r[0][:, lo:hi], acc[i, 0][:], bias[:, 0:1], 0.0, ALU.add, ALU.max)
+        lo, hi = spans[0]
+        nc.scalar.activation(y[0][:, lo:hi], r[0][:, lo:hi], ACT.Square)
+        for i in (2, 1):
+            lo, hi = spans[i]
+            nc.vector.tensor_tensor(y[0][:, lo:hi], r[0][:, lo:hi], r[0][:, lo:hi], ALU.mult)
+        for i in order:
+            lo, hi = spans[i]
+            nc.scalar.activation(r[1][:, lo:hi], acc[i, 1][:], ACT.Relu, bias=bias[:, 1:2])
+        nc.scalar.activation(y[1][:], r[1][:], ACT.Square)
+
+        terms = [sb.tile([P, D, V], F32, name=f"terms{c}", align_bytes=64) for c in range(2)]
+        part = [sb.tile([P, V], F32, name=f"part{c}", align_bytes=64) for c in range(2)]
+        res = [sb.tile([P, V], F32, name=f"res{c}", align_bytes=64) for c in range(2)]
+
+        def fetch(c, d, lo, hi):
+            nc.vector.tensor_tensor(terms[c][:, d, lo:hi], y[c][:].indirect(pos_t[d][:, lo // G:hi // G]), gates[c][:, d, lo:hi], ALU.mult)
+
+        def finish(c, lo, hi):
+            nc.vector.tensor_tensor(res[c][:, lo:hi], part[c][:, lo:hi], terms[c][:, 2, lo:hi], ALU.add)
+            nc.sync.dma_start(out[c * P:(c + 1) * P, lo:hi], res[c][:, lo:hi])
+
+        for d in range(D):
+            fetch(0, d, 0, V)
+        nc.vector.tensor_tensor(part[0][:], terms[0][:, 0, :], terms[0][:, 1, :], ALU.add)
+        fetch(1, 0, 0, V)
+        finish(0, 0, V)
+        fetch(1, 1, 0, V)
+        fetch(1, 2, 0, P)
+        nc.vector.tensor_tensor(part[1][:], terms[1][:, 0, :], terms[1][:, 1, :], ALU.add)
+        fetch(1, 2, P, V)
+        finish(1, 0, P)
+        finish(1, P, V)

@@ -1,6 +1,7 @@
 from contextlib import ExitStack
 
 import concourse.mybir as mybir
+from concourse.masks import make_identity
 
 K, T, D, S, V, N = 512, 1024, 3, 512, 256, 256
 FLOPS = 2 * K * S * N
@@ -41,6 +42,9 @@ def tile_picked_sub_lin_relu2_sub_e_kernel(tc, xT, w_words, w_scales, b, gate, o
         nc.sync.dma_start(offs_t[:], offs)
         for j in range(1, 4):
             nc.sync.dma_start(x[j][:], x_rows[:, j, :])
+        nc.vector.memset(w_plane[:].bitcast(I32), 0)
+        for q in range(4):
+            nc.sync.dma_start(w_plane[32 * q:32 * q + 4, :].bitcast(I32), w_scales[0, 4 * q:4 * q + 4, :].bitcast(I32))
         nc.sync.dma_start(w_codes[:], w_words[0].rearrange("p n t -> p (n t)").bitcast(I32))
         with nc.allow_non_contiguous_dma(reason="one bias value to a partition"):
             nc.sync.dma_start(bias[:], b.rearrange("(c p) o -> p (c o)", p=P))
@@ -51,87 +55,102 @@ def tile_picked_sub_lin_relu2_sub_e_kernel(tc, xT, w_words, w_scales, b, gate, o
 
         nc.vector.memset(warm[:], 0.0)
         nc.scalar.activation(warm_out[:], warm[:], ACT.Square)
-        nc.gpsimd.memset(w_plane[:], 0)
-        for q in range(4):
-            nc.gpsimd.dma_start(w_plane[32 * q:32 * q + 4, :].bitcast(I32), w_scales[0, 4 * q:4 * q + 4, :].bitcast(I32))
+
+        ident = sb.tile([P, P], F32, name="ident", align_bytes=64)
+        make_identity(nc, ident[:])
 
         def picks(lo, hi):
             return offs_t[:, lo // G:hi // G]
 
-        spans = [(0, 256), (256, 384), (384, 512)]
-        packed = [sb.tile([P, hi - lo, 4], BF16, name=f"packed{i}", align_bytes=64) for i, (lo, hi) in enumerate(spans)]
+        H = S // 2
+        packed = [sb.tile([P, P, 4], BF16, name="packed0", align_bytes=64),
+                  sb.tile([P, P, 4], BF16, name="packed1", align_bytes=64),
+                  sb.tile([P, H, 4], BF16, name="packed2", align_bytes=64)]
+        spans = [(0, P), (P, H), (H, S)]
         g01 = sb.tile([P, 2, S], F32, name="g01", align_bytes=64)
-        g23 = sb.tile([P, 2, 384], F32, name="g23", align_bytes=64)
+        g23 = sb.tile([P, 2, H], F32, name="g23", align_bytes=64)
 
         nc.vector.tensor_copy(g01[:, 0, :], x[0][:].indirect(offs_t[:]))
-        for lo, hi in ((0, 256), (256, 512)):
+        for lo, hi in ((0, H), (H, S)):
             nc.vector.tensor_copy(g01[:, 1, lo:hi], x[1][:].indirect(picks(lo, hi)))
         for i, (lo, hi) in enumerate(spans):
             nc.scalar.copy(packed[i][:, :, 0:2], g01[:, :, lo:hi].rearrange("p u n -> p n u"))
-        nc.vector.tensor_copy(g23[:, 0, :], x[2][:].indirect(picks(0, 384)))
-        nc.vector.tensor_copy(packed[2][:, :, 2], x[2][:].indirect(picks(384, 512)))
-        for lo in (0, 128, 256):
+        nc.vector.tensor_copy(g23[:, 0, :], x[2][:].indirect(picks(0, H)))
+        nc.vector.tensor_copy(packed[2][:, :, 2], x[2][:].indirect(picks(H, S)))
+        for lo in (0, P):
             nc.vector.tensor_copy(g23[:, 1, lo:lo + P], x[3][:].indirect(picks(lo, lo + P)))
-        nc.vector.tensor_copy(packed[2][:, :, 3], x[3][:].indirect(picks(384, 512)))
-        for i, at, lo in ((0, 0, 0), (0, 128, 128), (1, 0, 256)):
-            nc.scalar.copy(packed[i][:, at:at + P, 2:4], g23[:, :, lo:lo + P].rearrange("p u n -> p n u"))
+        for lo in (0, P):
+            nc.vector.tensor_copy(packed[2][:, lo:lo + P, 3], x[3][:].indirect(picks(H + lo, H + lo + P)))
+        for i in (0, 1):
+            nc.scalar.copy(packed[i][:, :, 2:4], g23[:, :, i * P:(i + 1) * P].rearrange("p u n -> p n u"))
 
-        order = (0, 2, 1)
-        codes, planes, acc = {}, {}, {}
+        codes = sb.tile([P, S], U32, name="codes", align_bytes=64)
+        plane = sb.tile([P, S], U8, name="plane", align_bytes=64)
+        sources = {0: packed[0][:], 1: packed[1][:], 2: packed[2][:, 0:P, :], 3: packed[2][:, P:H, :]}
+        order = (0, 2, 3, 1)
         for i in order:
-            n = spans[i][1] - spans[i][0]
-            codes[i] = sb.tile([P, n], U32, name=f"codes{i}", align_bytes=64)
-            planes[i] = sb.tile([P, n], U8, name=f"planes{i}", align_bytes=64)
-            nc.vector.quantize_mx(out=codes[i][:].bitcast(FP8X4), scales=planes[i][:], in_=packed[i][:].rearrange("p n j -> p (n j)"))
-        for i, c in ((0, 0), (2, 0), (0, 1), (1, 0), (2, 1), (1, 1)):
-            n = spans[i][1] - spans[i][0]
-            acc[i, c] = psum.tile([P, n], F32, name=f"acc{i}_{c}")
+            cols = slice(i * P, (i + 1) * P)
+            nc.vector.quantize_mx(out=codes[:, cols].bitcast(FP8X4), scales=plane[:, cols], in_=sources[i].rearrange("p n j -> p (n j)"))
+
+        def product(acc, c, cols):
             nc.tensor.matmul_mx(
-                out=acc[i, c][:],
+                out=acc,
                 lhsT=w_codes[:, c * P:(c + 1) * P].bitcast(FP8X4),
                 lhsT_scale=w_plane[:, c * P:(c + 1) * P],
-                rhs=codes[i][:].bitcast(FP8X4),
-                rhs_scale=planes[i][:],
+                rhs=codes[:, cols].bitcast(FP8X4),
+                rhs_scale=plane[:, cols],
                 start=True,
                 stop=True,
             )
 
+        acc0 = {}
+        for i in order:
+            acc0[i] = psum.tile([P, P], F32, name=f"acc0_{i}")
+            product(acc0[i][:], 0, slice(i * P, (i + 1) * P))
+        acc1 = psum.tile([P, S], F32, name="acc1")
+        product(acc1[:], 1, slice(0, S))
+
         r = [sb.tile([P, S], F32, name=f"r{c}", align_bytes=64) for c in range(2)]
         y = [sb.tile([P, S], F32, name=f"y{c}", align_bytes=64) for c in range(2)]
-        lo, hi = spans[0]
-        nc.scalar.activation(r[0][:, lo:hi], acc[0, 0][:], ACT.Relu, bias=bias[:, 0:1])
+        for i in (0, 3):
+            cols = slice(i * P, (i + 1) * P)
+            nc.scalar.activation(r[0][:, cols], acc0[i][:], ACT.Relu, bias=bias[:, 0:1])
+            nc.scalar.activation(y[0][:, cols], r[0][:, cols], ACT.Square)
         for i in (2, 1):
-            lo, hi = spans[i]
-            nc.vector.tensor_scalar(r[0][:, lo:hi], acc[i, 0][:], bias[:, 0:1], 0.0, ALU.add, ALU.max)
-        lo, hi = spans[0]
-        nc.scalar.activation(y[0][:, lo:hi], r[0][:, lo:hi], ACT.Square)
+            cols = slice(i * P, (i + 1) * P)
+            nc.vector.tensor_scalar(r[0][:, cols], acc0[i][:], bias[:, 0:1], 0.0, ALU.add, ALU.max)
         for i in (2, 1):
-            lo, hi = spans[i]
-            nc.vector.tensor_tensor(y[0][:, lo:hi], r[0][:, lo:hi], r[0][:, lo:hi], ALU.mult)
-        for i in order:
-            lo, hi = spans[i]
-            nc.scalar.activation(r[1][:, lo:hi], acc[i, 1][:], ACT.Relu, bias=bias[:, 1:2])
+            cols = slice(i * P, (i + 1) * P)
+            nc.vector.tensor_tensor(y[0][:, cols], r[0][:, cols], r[0][:, cols], ALU.mult)
+        nc.scalar.activation(r[1][:], acc1[:], ACT.Relu, bias=bias[:, 1:2])
         nc.scalar.activation(y[1][:], r[1][:], ACT.Square)
 
         terms = [sb.tile([P, D, V], F32, name=f"terms{c}", align_bytes=64) for c in range(2)]
-        part = [sb.tile([P, V], F32, name=f"part{c}", align_bytes=64) for c in range(2)]
+        part = sb.tile([P, V], F32, name="part", align_bytes=64)
         res = [sb.tile([P, V], F32, name=f"res{c}", align_bytes=64) for c in range(2)]
 
         def fetch(c, d, lo, hi):
             nc.vector.tensor_tensor(terms[c][:, d, lo:hi], y[c][:].indirect(pos_t[d][:, lo // G:hi // G]), gates[c][:, d, lo:hi], ALU.mult)
 
-        def finish(c, lo, hi):
-            nc.vector.tensor_tensor(res[c][:, lo:hi], part[c][:, lo:hi], terms[c][:, 2, lo:hi], ALU.add)
-            nc.sync.dma_start(out[c * P:(c + 1) * P, lo:hi], res[c][:, lo:hi])
-
+        turned = [psum.tile([P, P], F32, name=f"turned{h}") for h in range(2)]
         for d in range(D):
             fetch(0, d, 0, V)
-        nc.vector.tensor_tensor(part[0][:], terms[0][:, 0, :], terms[0][:, 1, :], ALU.add)
+            for h in range(2):
+                nc.tensor.matmul(turned[h][:], terms[0][:, d, h * P:(h + 1) * P], ident[:], start=(d == 0), stop=(d == D - 1), is_transpose=True)
+        turned_sb = sb.tile([P, 2, P], F32, name="turned_sb", align_bytes=64)
+        back = psum.tile([P, V], F32, name="back")
+        for h in range(2):
+            nc.scalar.copy(turned_sb[:, h, :], turned[h][:])
+        for h in range(2):
+            nc.tensor.transpose(back[:, h * P:(h + 1) * P], turned_sb[:, h, :], ident[:])
+        nc.scalar.copy(res[0][:], back[:])
+        nc.sync.dma_start(out[0:P, :], res[0][:])
+
         fetch(1, 0, 0, V)
-        finish(0, 0, V)
         fetch(1, 1, 0, V)
-        fetch(1, 2, 0, P)
-        nc.vector.tensor_tensor(part[1][:], terms[1][:, 0, :], terms[1][:, 1, :], ALU.add)
-        fetch(1, 2, P, V)
-        finish(1, 0, P)
-        finish(1, P, V)
+        fetch(1, 2, 0, 192)
+        nc.vector.tensor_tensor(part[:], terms[1][:, 0, :], terms[1][:, 1, :], ALU.add)
+        fetch(1, 2, 192, V)
+        for lo, hi in ((0, 192), (192, V)):
+            nc.vector.tensor_tensor(res[1][:, lo:hi], part[:, lo:hi], terms[1][:, 2, lo:hi], ALU.add)
+            nc.sync.dma_start(out[P:N, lo:hi], res[1][:, lo:hi])

@@ -38,26 +38,29 @@ def tile_picked_sub_lin_relu2_sub_e_kernel(tc, xT, w_words, w_scales, b, gate, o
         warm = sb.tile([P, 8], F32, name="warm")
         warm_out = sb.tile([P, 8], F32, name="warm_out")
 
+        ident = sb.tile([P, P], F32, name="ident", align_bytes=64)
+        nc.vector.memset(warm[:], 0.0)
+        nc.vector.memset(w_plane[:].bitcast(I32), 0)
+        make_identity(nc, ident[:])
+        nc.scalar.activation(warm_out[:], warm[:], ACT.Square)
+
+        def load_gates(c):
+            nc.sync.dma_start(gates[c][:], gate[:, c * P:(c + 1) * P, :].rearrange("d p v -> p d v"))
+
         nc.sync.dma_start(x[0][:], x_rows[:, 0, :])
         nc.sync.dma_start(offs_t[:], offs)
         for j in range(1, 4):
             nc.sync.dma_start(x[j][:], x_rows[:, j, :])
-        nc.vector.memset(w_plane[:].bitcast(I32), 0)
-        for q in range(4):
-            nc.sync.dma_start(w_plane[32 * q:32 * q + 4, :].bitcast(I32), w_scales[0, 4 * q:4 * q + 4, :].bitcast(I32))
         nc.sync.dma_start(w_codes[:], w_words[0].rearrange("p n t -> p (n t)").bitcast(I32))
+        for q in range(4):
+            nc.scalar.dma_start(w_plane[32 * q:32 * q + 4, :].bitcast(I32), w_scales[0, 4 * q:4 * q + 4, :].bitcast(I32))
         with nc.allow_non_contiguous_dma(reason="one bias value to a partition"):
             nc.sync.dma_start(bias[:], b.rearrange("(c p) o -> p (c o)", p=P))
-        for d, pos in enumerate((pos1, pos2, pos3)):
-            nc.sync.dma_start(pos_t[d][:], pos)
-        for c in range(2):
-            nc.sync.dma_start(gates[c][:], gate[:, c * P:(c + 1) * P, :].rearrange("d p v -> p d v"))
-
-        nc.vector.memset(warm[:], 0.0)
-        nc.scalar.activation(warm_out[:], warm[:], ACT.Square)
-
-        ident = sb.tile([P, P], F32, name="ident", align_bytes=64)
-        make_identity(nc, ident[:])
+        nc.sync.dma_start(pos_t[0][:], pos1)
+        load_gates(0)
+        nc.sync.dma_start(pos_t[1][:], pos2)
+        nc.sync.dma_start(pos_t[2][:], pos3)
+        load_gates(1)
 
         def picks(lo, hi):
             return offs_t[:, lo // G:hi // G]
@@ -105,7 +108,7 @@ def tile_picked_sub_lin_relu2_sub_e_kernel(tc, xT, w_words, w_scales, b, gate, o
 
         acc0 = {}
         for i in order:
-            acc0[i] = psum.tile([P, P], F32, name=f"acc0_{i}")
+            acc0[i] = psum.tile([P, P], F32, name=f"acc0_{i}", tag=f"acc0_{i}")
             product(acc0[i][:], 0, slice(i * P, (i + 1) * P))
         acc1 = psum.tile([P, S], F32, name="acc1")
         product(acc1[:], 1, slice(0, S))
@@ -132,19 +135,27 @@ def tile_picked_sub_lin_relu2_sub_e_kernel(tc, xT, w_words, w_scales, b, gate, o
         def fetch(c, d, lo, hi):
             nc.vector.tensor_tensor(terms[c][:, d, lo:hi], y[c][:].indirect(pos_t[d][:, lo // G:hi // G]), gates[c][:, d, lo:hi], ALU.mult)
 
-        turned = [psum.tile([P, P], F32, name=f"turned{h}") for h in range(2)]
-        for d in range(D):
+        turned = [psum.tile([P, P], F32, name=f"turned{h}", tag=f"turned{h}") for h in range(2)]
+
+        def turn(d, h):
+            nc.tensor.matmul(turned[h][:], terms[0][:, d, h * P:(h + 1) * P], ident[:], start=(d == 0), stop=(d == D - 1), is_transpose=True)
+
+        for d in range(D - 1):
             fetch(0, d, 0, V)
             for h in range(2):
-                nc.tensor.matmul(turned[h][:], terms[0][:, d, h * P:(h + 1) * P], ident[:], start=(d == 0), stop=(d == D - 1), is_transpose=True)
+                turn(d, h)
+        for h in range(2):
+            fetch(0, D - 1, h * P, (h + 1) * P)
+            turn(D - 1, h)
         turned_sb = sb.tile([P, 2, P], F32, name="turned_sb", align_bytes=64)
-        back = psum.tile([P, V], F32, name="back")
+        back = [psum.tile([P, P], F32, name=f"back{h}", tag=f"acc0_{h}") for h in range(2)]
         for h in range(2):
             nc.scalar.copy(turned_sb[:, h, :], turned[h][:])
+            nc.tensor.transpose(back[h][:], turned_sb[:, h, :], ident[:])
         for h in range(2):
-            nc.tensor.transpose(back[:, h * P:(h + 1) * P], turned_sb[:, h, :], ident[:])
-        nc.scalar.copy(res[0][:], back[:])
-        nc.sync.dma_start(out[0:P, :], res[0][:])
+            cols = slice(h * P, (h + 1) * P)
+            nc.scalar.copy(res[0][:, cols], back[h][:])
+            nc.scalar.dma_start(out[0:P, cols], res[0][:, cols])
 
         fetch(1, 0, 0, V)
         fetch(1, 1, 0, V)

@@ -33,7 +33,7 @@ def tile_picked_sub_lin_relu2_sub_e_kernel(tc, xT, w_words, w_scales, b, gate, o
         x = [sb.tile([P, T], F32, name=f"x{j}", align_bytes=64) for j in range(4)]
         w_codes = sb.tile([P, N], I32, name="w_codes", align_bytes=64)
         w_plane = sb.tile([P, N], U8, name="w_plane", align_bytes=64)
-        bias = sb.tile([P, 2], F32, name="bias")
+        bias = sb.tile([P, 2, 8], F32, name="bias")
         gates = [sb.tile([P, D, V], F32, name=f"gates{c}", align_bytes=64) for c in range(2)]
         warm = sb.tile([P, 8], F32, name="warm")
         warm_out = sb.tile([P, 8], F32, name="warm_out")
@@ -55,7 +55,7 @@ def tile_picked_sub_lin_relu2_sub_e_kernel(tc, xT, w_words, w_scales, b, gate, o
         for q in range(4):
             nc.scalar.dma_start(w_plane[32 * q:32 * q + 4, :].bitcast(I32), w_scales[0, 4 * q:4 * q + 4, :].bitcast(I32))
         with nc.allow_non_contiguous_dma(reason="one bias value to a partition"):
-            nc.sync.dma_start(bias[:], b.rearrange("(c p) o -> p (c o)", p=P))
+            nc.sync.dma_start(bias[:, :, 0:1], b.rearrange("(c p) o -> p c o", p=P))
         nc.sync.dma_start(pos_t[0][:], pos1)
         load_gates(0)
         nc.sync.dma_start(pos_t[1][:], pos2)
@@ -115,17 +115,19 @@ def tile_picked_sub_lin_relu2_sub_e_kernel(tc, xT, w_words, w_scales, b, gate, o
 
         r = [sb.tile([P, S], F32, name=f"r{c}", align_bytes=64) for c in range(2)]
         y = [sb.tile([P, S], F32, name=f"y{c}", align_bytes=64) for c in range(2)]
-        for i in (0, 3):
+        for i in (0, 2):
             cols = slice(i * P, (i + 1) * P)
-            nc.scalar.activation(r[0][:, cols], acc0[i][:], ACT.Relu, bias=bias[:, 0:1])
+            nc.scalar.activation(r[0][:, cols], acc0[i][:], ACT.Relu, bias=bias[:, 0, 0:1])
+        for i in (0, 2):
+            cols = slice(i * P, (i + 1) * P)
             nc.scalar.activation(y[0][:, cols], r[0][:, cols], ACT.Square)
-        for i in (2, 1):
+        for i in (3, 1):
             cols = slice(i * P, (i + 1) * P)
-            nc.vector.tensor_scalar(r[0][:, cols], acc0[i][:], bias[:, 0:1], 0.0, ALU.add, ALU.max)
-        for i in (2, 1):
+            nc.vector.tensor_scalar(r[0][:, cols], acc0[i][:], bias[:, 0, 0:1], 0.0, ALU.add, ALU.max)
+        for i in (3, 1):
             cols = slice(i * P, (i + 1) * P)
             nc.vector.tensor_tensor(y[0][:, cols], r[0][:, cols], r[0][:, cols], ALU.mult)
-        nc.scalar.activation(r[1][:], acc1[:], ACT.Relu, bias=bias[:, 1:2])
+        nc.scalar.activation(r[1][:], acc1[:], ACT.Relu, bias=bias[:, 1, 0:1])
         nc.scalar.activation(y[1][:], r[1][:], ACT.Square)
 
         terms = [sb.tile([P, D, V], F32, name=f"terms{c}", align_bytes=64) for c in range(2)]

@@ -34,7 +34,8 @@ def tile_picked_sub_lin_relu2_sub_e_kernel(tc, xT, w_words, w_scales, b, gate, o
         w_codes = sb.tile([P, N], I32, name="w_codes", align_bytes=64)
         w_plane = sb.tile([P, N], U8, name="w_plane", align_bytes=64)
         bias = sb.tile([P, 2, 8], F32, name="bias")
-        gates = [sb.tile([P, D, V], F32, name=f"gates{c}", align_bytes=64) for c in range(2)]
+        gates = sb.tile([P, D, V], F32, name="gates", align_bytes=64)
+        gate_col = sb.tile([P, 2, 8], F32, name="gate_col")
         warm = sb.tile([P, 8], F32, name="warm")
         warm_out = sb.tile([P, 8], F32, name="warm_out")
 
@@ -43,9 +44,6 @@ def tile_picked_sub_lin_relu2_sub_e_kernel(tc, xT, w_words, w_scales, b, gate, o
         nc.vector.memset(w_plane[:].bitcast(I32), 0)
         make_identity(nc, ident[:])
         nc.scalar.activation(warm_out[:], warm[:], ACT.Square)
-
-        def load_gates(c):
-            nc.sync.dma_start(gates[c][:], gate[:, c * P:(c + 1) * P, :].rearrange("d p v -> p d v"))
 
         nc.sync.dma_start(x[0][:], x_rows[:, 0, :])
         nc.sync.dma_start(offs_t[:], offs)
@@ -57,10 +55,11 @@ def tile_picked_sub_lin_relu2_sub_e_kernel(tc, xT, w_words, w_scales, b, gate, o
         with nc.allow_non_contiguous_dma(reason="one bias value to a partition"):
             nc.sync.dma_start(bias[:, :, 0:1], b.rearrange("(c p) o -> p c o", p=P))
         nc.sync.dma_start(pos_t[0][:], pos1)
-        load_gates(0)
         nc.sync.dma_start(pos_t[1][:], pos2)
         nc.sync.dma_start(pos_t[2][:], pos3)
-        load_gates(1)
+        nc.sync.dma_start(gates[:], gate[:, 0:P, :].rearrange("d p v -> p d v"))
+        with nc.allow_non_contiguous_dma(reason="one gate value to a partition"):
+            nc.sync.dma_start(gate_col[:, :, 0:1], gate[0, 0:1, :].rearrange("o (h p) -> p h o", p=P))
 
         def picks(lo, hi):
             return offs_t[:, lo // G:hi // G]
@@ -110,8 +109,9 @@ def tile_picked_sub_lin_relu2_sub_e_kernel(tc, xT, w_words, w_scales, b, gate, o
         for i in order:
             acc0[i] = psum.tile([P, P], F32, name=f"acc0_{i}", tag=f"acc0_{i}")
             product(acc0[i][:], 0, slice(i * P, (i + 1) * P))
-        acc1 = psum.tile([P, S], F32, name="acc1")
-        product(acc1[:], 1, slice(0, S))
+        acc1 = [psum.tile([P, H], F32, name=f"acc1_{h}") for h in range(2)]
+        for h in range(2):
+            product(acc1[h][:], 1, slice(h * H, (h + 1) * H))
 
         r = [sb.tile([P, S], F32, name=f"r{c}", align_bytes=64) for c in range(2)]
         y = [sb.tile([P, S], F32, name=f"y{c}", align_bytes=64) for c in range(2)]
@@ -124,36 +124,40 @@ def tile_picked_sub_lin_relu2_sub_e_kernel(tc, xT, w_words, w_scales, b, gate, o
         for i in (3, 1):
             cols = slice(i * P, (i + 1) * P)
             nc.vector.tensor_scalar(r[0][:, cols], acc0[i][:], bias[:, 0, 0:1], 0.0, ALU.add, ALU.max)
-        for i in (3, 1):
-            cols = slice(i * P, (i + 1) * P)
-            nc.vector.tensor_tensor(y[0][:, cols], r[0][:, cols], r[0][:, cols], ALU.mult)
-        nc.scalar.activation(r[1][:], acc1[:], ACT.Relu, bias=bias[:, 1, 0:1])
-        nc.scalar.activation(y[1][:], r[1][:], ACT.Square)
+        nc.vector.tensor_tensor(y[0][:, 3 * P:S], r[0][:, 3 * P:S], r[0][:, 3 * P:S], ALU.mult)
+        nc.scalar.activation(y[0][:, P:H], r[0][:, P:H], ACT.Square)
+        for h in range(2):
+            nc.scalar.activation(r[1][:, h * H:(h + 1) * H], acc1[h][:], ACT.Relu, bias=bias[:, 1, 0:1])
+        for h in range(2):
+            nc.scalar.activation(y[1][:, h * H:(h + 1) * H], r[1][:, h * H:(h + 1) * H], ACT.Square)
 
         terms = [sb.tile([P, D, V], F32, name=f"terms{c}", align_bytes=64) for c in range(2)]
         part = sb.tile([P, V], F32, name="part", align_bytes=64)
         res = [sb.tile([P, V], F32, name=f"res{c}", align_bytes=64) for c in range(2)]
 
         def fetch(c, d, lo, hi):
-            nc.vector.tensor_tensor(terms[c][:, d, lo:hi], y[c][:].indirect(pos_t[d][:, lo // G:hi // G]), gates[c][:, d, lo:hi], ALU.mult)
+            nc.vector.tensor_tensor(terms[c][:, d, lo:hi], y[c][:].indirect(pos_t[d][:, lo // G:hi // G]), gates[:, d, lo:hi], ALU.mult)
 
+        unsquared = sb.tile([P, V], F32, name="unsquared", align_bytes=64)
+        turned_sb = sb.tile([P, 2, 2, P], F32, name="turned_sb", align_bytes=64)
+        first = psum.tile([P, 2, P], F32, name="first", tag="acc0_0")
         turned = [psum.tile([P, P], F32, name=f"turned{h}", tag=f"turned{h}") for h in range(2)]
-
-        def turn(d, h):
-            nc.tensor.matmul(turned[h][:], terms[0][:, d, h * P:(h + 1) * P], ident[:], start=(d == 0), stop=(d == D - 1), is_transpose=True)
-
-        for d in range(D - 1):
+        back = [psum.tile([P, P], F32, name=f"back{h}", tag=f"acc0_{2 + h}") for h in range(2)]
+        nc.vector.tensor_copy(unsquared[:], r[0][:].indirect(pos_t[0][:]))
+        nc.scalar.activation(terms[0][:, 0, :], unsquared[:], ACT.Square)
+        for h in range(2):
+            nc.tensor.transpose(first[:, h, :], terms[0][:, 0, h * P:(h + 1) * P], ident[:])
+        for h in range(2):
+            nc.scalar.activation(turned_sb[:, 0, h, :], first[:, h, :], ACT.Copy, scale=gate_col[:, h, 0:1])
+        for d in (1, 2):
             fetch(0, d, 0, V)
             for h in range(2):
-                turn(d, h)
+                nc.tensor.matmul(turned[h][:], terms[0][:, d, h * P:(h + 1) * P], ident[:], start=(d == 1), stop=(d == 2), is_transpose=True)
         for h in range(2):
-            fetch(0, D - 1, h * P, (h + 1) * P)
-            turn(D - 1, h)
-        turned_sb = sb.tile([P, 2, P], F32, name="turned_sb", align_bytes=64)
-        back = [psum.tile([P, P], F32, name=f"back{h}", tag=f"acc0_{h}") for h in range(2)]
+            nc.scalar.copy(turned_sb[:, 1, h, :], turned[h][:])
         for h in range(2):
-            nc.scalar.copy(turned_sb[:, h, :], turned[h][:])
-            nc.tensor.transpose(back[h][:], turned_sb[:, h, :], ident[:])
+            for e in range(2):
+                nc.tensor.matmul(back[h][:], turned_sb[:, e, h, :], ident[:], start=(e == 0), stop=(e == 1), is_transpose=True)
         for h in range(2):
             cols = slice(h * P, (h + 1) * P)
             nc.scalar.copy(res[0][:, cols], back[h][:])

@@ -109,9 +109,8 @@ def tile_picked_sub_lin_relu2_sub_e_kernel(tc, xT, w_words, w_scales, b, gate, o
         for i in order:
             acc0[i] = psum.tile([P, P], F32, name=f"acc0_{i}", tag=f"acc0_{i}")
             product(acc0[i][:], 0, slice(i * P, (i + 1) * P))
-        acc1 = [psum.tile([P, H], F32, name=f"acc1_{h}") for h in range(2)]
-        for h in range(2):
-            product(acc1[h][:], 1, slice(h * H, (h + 1) * H))
+        acc1 = [psum.tile([P, H], F32, name="acc1_0")]
+        product(acc1[0][:], 1, slice(0, H))
 
         r = [sb.tile([P, S], F32, name=f"r{c}", align_bytes=64) for c in range(2)]
         y = [sb.tile([P, S], F32, name=f"y{c}", align_bytes=64) for c in range(2)]
@@ -126,6 +125,8 @@ def tile_picked_sub_lin_relu2_sub_e_kernel(tc, xT, w_words, w_scales, b, gate, o
             nc.vector.tensor_scalar(r[0][:, cols], acc0[i][:], bias[:, 0, 0:1], 0.0, ALU.add, ALU.max)
         nc.vector.tensor_tensor(y[0][:, 3 * P:S], r[0][:, 3 * P:S], r[0][:, 3 * P:S], ALU.mult)
         nc.scalar.activation(y[0][:, P:H], r[0][:, P:H], ACT.Square)
+        acc1.append(psum.tile([P, H], F32, name="acc1_1", tag="acc0_1"))
+        product(acc1[1][:], 1, slice(H, S))
         for h in range(2):
             nc.scalar.activation(r[1][:, h * H:(h + 1) * H], acc1[h][:], ACT.Relu, bias=bias[:, 1, 0:1])
         for h in range(2):

@@ -45,9 +45,9 @@ def tile_picked_sub_lin_relu2_sub_e_kernel(tc, xT, w_words, w_scales, b, gate, o
         make_identity(nc, ident[:])
         nc.scalar.activation(warm_out[:], warm[:], ACT.Square)
 
-        nc.sync.dma_start(x[0][:], x_rows[:, 0, :])
+        nc.sync.dma_start(x[2][:], x_rows[:, 2, :])
         nc.sync.dma_start(offs_t[:], offs)
-        for j in range(1, 4):
+        for j in (0, 1, 3):
             nc.sync.dma_start(x[j][:], x_rows[:, j, :])
         nc.sync.dma_start(w_codes[:], w_words[0].rearrange("p n t -> p (n t)").bitcast(I32))
         for q in range(4):
@@ -65,34 +65,34 @@ def tile_picked_sub_lin_relu2_sub_e_kernel(tc, xT, w_words, w_scales, b, gate, o
             return offs_t[:, lo // G:hi // G]
 
         H = S // 2
-        packed = [sb.tile([P, P, 4], BF16, name="packed0", align_bytes=64),
-                  sb.tile([P, P, 4], BF16, name="packed1", align_bytes=64),
-                  sb.tile([P, H, 4], BF16, name="packed2", align_bytes=64)]
-        spans = [(0, P), (P, H), (H, S)]
-        g01 = sb.tile([P, 2, S], F32, name="g01", align_bytes=64)
-        g23 = sb.tile([P, 2, H], F32, name="g23", align_bytes=64)
+        W = 192
+        woven = [(0, P), (P, W)]
+        packed = [sb.tile([P, hi - lo, 4], BF16, name=f"packed{lo}", align_bytes=64) for lo, hi in woven]
+        direct = sb.tile([P, S - W, 4], BF16, name="direct", align_bytes=64)
+        rows = sb.tile([P, 4, S], BF16, name="rows", align_bytes=64)
+        x0_rounded = sb.tile([P, T], BF16, name="x0_rounded", align_bytes=64)
 
-        nc.vector.tensor_copy(g01[:, 0, :], x[0][:].indirect(offs_t[:]))
-        for lo, hi in ((0, H), (H, S)):
-            nc.vector.tensor_copy(g01[:, 1, lo:hi], x[1][:].indirect(picks(lo, hi)))
-        for i, (lo, hi) in enumerate(spans):
-            nc.scalar.copy(packed[i][:, :, 0:2], g01[:, :, lo:hi].rearrange("p u n -> p n u"))
-        nc.vector.tensor_copy(g23[:, 0, :], x[2][:].indirect(picks(0, H)))
-        nc.vector.tensor_copy(packed[2][:, :, 2], x[2][:].indirect(picks(H, S)))
-        for lo in (0, P):
-            nc.vector.tensor_copy(g23[:, 1, lo:lo + P], x[3][:].indirect(picks(lo, lo + P)))
-        for lo in (0, P):
-            nc.vector.tensor_copy(packed[2][:, lo:lo + P, 3], x[3][:].indirect(picks(H + lo, H + lo + P)))
-        for i in (0, 1):
-            nc.scalar.copy(packed[i][:, :, 2:4], g23[:, :, i * P:(i + 1) * P].rearrange("p u n -> p n u"))
+        nc.vector.tensor_copy(rows[:, 2, 0:W], x[2][:].indirect(picks(0, W)))
+        nc.vector.tensor_copy(direct[:, :, 2], x[2][:].indirect(picks(W, S)))
+        nc.scalar.copy(x0_rounded[:], x[0][:])
+        nc.scalar.activation(rows[:, 0, 0:W], x0_rounded[:].indirect(picks(0, W)), ACT.Copy)
+        nc.vector.tensor_copy(rows[:, 0, W:S], x[0][:].indirect(picks(W, S)))
+        for lo, hi in ((W, S), (0, W)):
+            nc.vector.tensor_copy(rows[:, 1, lo:hi], x[1][:].indirect(picks(lo, hi)))
+        nc.scalar.copy(direct[:, :, 0:2], rows[:, 0:2, W:S].rearrange("p u n -> p n u"))
+        for lo, hi in woven:
+            nc.vector.tensor_copy(rows[:, 3, lo:hi], x[3][:].indirect(picks(lo, hi)))
+        for lo, hi in ((W, 3 * P), (3 * P, S)):
+            nc.vector.tensor_copy(direct[:, lo - W:hi - W, 3], x[3][:].indirect(picks(lo, hi)))
+        for i, (lo, hi) in enumerate(woven):
+            nc.scalar.copy(packed[i][:].rearrange("p (c n) t -> p c t n", n=4), rows[:, :, lo:hi].rearrange("p t (c n) -> p c t n", n=4))
 
         codes = sb.tile([P, S], U32, name="codes", align_bytes=64)
         plane = sb.tile([P, S], U8, name="plane", align_bytes=64)
-        sources = {0: packed[0][:], 1: packed[1][:], 2: packed[2][:, 0:P, :], 3: packed[2][:, P:H, :]}
-        order = (0, 2, 3, 1)
-        for i in order:
-            cols = slice(i * P, (i + 1) * P)
-            nc.vector.quantize_mx(out=codes[:, cols].bitcast(FP8X4), scales=plane[:, cols], in_=sources[i].rearrange("p n j -> p (n j)"))
+        pieces = [(slice(H, 3 * P), direct[:, H - W:3 * P - W, :]), (slice(W, H), direct[:, 0:H - W, :]), (slice(0, P), packed[0][:]),
+                  (slice(3 * P, S), direct[:, 3 * P - W:S - W, :]), (slice(P, W), packed[1][:])]
+        for cols, source in pieces:
+            nc.vector.quantize_mx(out=codes[:, cols].bitcast(FP8X4), scales=plane[:, cols], in_=source.rearrange("p n j -> p (n j)"))
 
         def product(acc, c, cols):
             nc.tensor.matmul_mx(
@@ -105,27 +105,24 @@ def tile_picked_sub_lin_relu2_sub_e_kernel(tc, xT, w_words, w_scales, b, gate, o
                 stop=True,
             )
 
-        acc0 = {}
-        for i in order:
-            acc0[i] = psum.tile([P, P], F32, name=f"acc0_{i}", tag=f"acc0_{i}")
-            product(acc0[i][:], 0, slice(i * P, (i + 1) * P))
+        spans = [slice(i * P, (i + 1) * P) for i in (2, 0, 3, 1)]
+        acc0 = []
+        for i, cols in enumerate(spans):
+            acc0.append(psum.tile([P, cols.stop - cols.start], F32, name=f"acc0_{i}", tag=f"acc0_{i}"))
+            product(acc0[i][:], 0, cols)
         acc1 = [psum.tile([P, H], F32, name="acc1_0")]
         product(acc1[0][:], 1, slice(0, H))
 
         r = [sb.tile([P, S], F32, name=f"r{c}", align_bytes=64) for c in range(2)]
         y = [sb.tile([P, S], F32, name=f"y{c}", align_bytes=64) for c in range(2)]
-        for i in (0, 2):
-            cols = slice(i * P, (i + 1) * P)
-            nc.scalar.activation(r[0][:, cols], acc0[i][:], ACT.Relu, bias=bias[:, 0, 0:1])
-        for i in (0, 2):
-            cols = slice(i * P, (i + 1) * P)
-            nc.scalar.activation(y[0][:, cols], r[0][:, cols], ACT.Square)
-        for i in (3, 1):
-            cols = slice(i * P, (i + 1) * P)
-            nc.vector.tensor_scalar(r[0][:, cols], acc0[i][:], bias[:, 0, 0:1], 0.0, ALU.add, ALU.max)
-        nc.vector.tensor_tensor(y[0][:, 3 * P:S], r[0][:, 3 * P:S], r[0][:, 3 * P:S], ALU.mult)
+        for i in (0, 1, 2):
+            nc.scalar.activation(r[0][:, spans[i]], acc0[i][:], ACT.Relu, bias=bias[:, 0, 0:1])
+        for i in (0, 1, 2):
+            nc.scalar.activation(y[0][:, spans[i]], r[0][:, spans[i]], ACT.Square)
+        for i in (3,):
+            nc.vector.tensor_scalar(r[0][:, spans[i]], acc0[i][:], bias[:, 0, 0:1], 0.0, ALU.add, ALU.max)
         nc.scalar.activation(y[0][:, P:H], r[0][:, P:H], ACT.Square)
-        acc1.append(psum.tile([P, H], F32, name="acc1_1", tag="acc0_1"))
+        acc1.append(psum.tile([P, H], F32, name="acc1_1", tag="acc0_3"))
         product(acc1[1][:], 1, slice(H, S))
         for h in range(2):
             nc.scalar.activation(r[1][:, h * H:(h + 1) * H], acc1[h][:], ACT.Relu, bias=bias[:, 1, 0:1])
@@ -143,7 +140,7 @@ def tile_picked_sub_lin_relu2_sub_e_kernel(tc, xT, w_words, w_scales, b, gate, o
         turned_sb = sb.tile([P, 2, 2, P], F32, name="turned_sb", align_bytes=64)
         first = psum.tile([P, 2, P], F32, name="first", tag="acc0_0")
         turned = [psum.tile([P, P], F32, name=f"turned{h}", tag=f"turned{h}") for h in range(2)]
-        back = [psum.tile([P, P], F32, name=f"back{h}", tag=f"acc0_{2 + h}") for h in range(2)]
+        back = [psum.tile([P, P], F32, name=f"back{h}", tag=f"acc0_{1 + h}") for h in range(2)]
         nc.vector.tensor_copy(unsquared[:], r[0][:].indirect(pos_t[0][:]))
         nc.scalar.activation(terms[0][:, 0, :], unsquared[:], ACT.Square)
         for h in range(2):

@@ -32,7 +32,7 @@ def tile_picked_sub_lin_relu2_sub_e_kernel(tc, xT, w_words, w_scales, b, gate, o
         x_rows = xT.rearrange("(p j) t -> p j t", j=4)
         x = [sb.tile([P, T], F32, name=f"x{j}", align_bytes=64) for j in range(4)]
         w_codes = sb.tile([P, N], I32, name="w_codes", align_bytes=64)
-        w_plane = sb.tile([P, N], U8, name="w_plane", align_bytes=64)
+        plane = sb.tile([P, S], U8, name="plane", align_bytes=64)
         bias = sb.tile([P, 2, 8], F32, name="bias")
         gates = sb.tile([P, D, V], F32, name="gates", align_bytes=64)
         gate_col = sb.tile([P, 2, 8], F32, name="gate_col")
@@ -41,17 +41,16 @@ def tile_picked_sub_lin_relu2_sub_e_kernel(tc, xT, w_words, w_scales, b, gate, o
 
         ident = sb.tile([P, P], F32, name="ident", align_bytes=64)
         nc.vector.memset(warm[:], 0.0)
-        nc.vector.memset(w_plane[:].bitcast(I32), 0)
         make_identity(nc, ident[:])
         nc.scalar.activation(warm_out[:], warm[:], ACT.Square)
 
         nc.sync.dma_start(x[2][:], x_rows[:, 2, :])
         nc.sync.dma_start(offs_t[:], offs)
+        for q in range(4):
+            nc.sync.dma_start(plane[32 * q + 4:32 * q + 8, S - N:S].bitcast(I32), w_scales[0, 4 * q:4 * q + 4, :].bitcast(I32))
         for j in (0, 1, 3):
             nc.sync.dma_start(x[j][:], x_rows[:, j, :])
         nc.sync.dma_start(w_codes[:], w_words[0].rearrange("p n t -> p (n t)").bitcast(I32))
-        for q in range(4):
-            nc.scalar.dma_start(w_plane[32 * q:32 * q + 4, :].bitcast(I32), w_scales[0, 4 * q:4 * q + 4, :].bitcast(I32))
         with nc.allow_non_contiguous_dma(reason="one bias value to a partition"):
             nc.sync.dma_start(bias[:, :, 0:1], b.rearrange("(c p) o -> p c o", p=P))
         nc.sync.dma_start(pos_t[0][:], pos1)
@@ -88,7 +87,6 @@ def tile_picked_sub_lin_relu2_sub_e_kernel(tc, xT, w_words, w_scales, b, gate, o
             nc.scalar.copy(packed[i][:].rearrange("p (c n) t -> p c t n", n=4), rows[:, :, lo:hi].rearrange("p t (c n) -> p c t n", n=4))
 
         codes = sb.tile([P, S], U32, name="codes", align_bytes=64)
-        plane = sb.tile([P, S], U8, name="plane", align_bytes=64)
         pieces = [(slice(H, 3 * P), direct[:, H - W:3 * P - W, :]), (slice(W, H), direct[:, 0:H - W, :]), (slice(0, P), packed[0][:]),
                   (slice(3 * P, S), direct[:, 3 * P - W:S - W, :]), (slice(P, W), packed[1][:])]
         for cols, source in pieces:
@@ -98,7 +96,7 @@ def tile_picked_sub_lin_relu2_sub_e_kernel(tc, xT, w_words, w_scales, b, gate, o
             nc.tensor.matmul_mx(
                 out=acc,
                 lhsT=w_codes[:, c * P:(c + 1) * P].bitcast(FP8X4),
-                lhsT_scale=w_plane[:, c * P:(c + 1) * P],
+                lhsT_scale=plane[4:P, S - N + c * P:S - N + (c + 1) * P],
                 rhs=codes[:, cols].bitcast(FP8X4),
                 rhs_scale=plane[:, cols],
                 start=True,

@@ -44,12 +44,14 @@ def tile_picked_sub_lin_relu2_sub_e_kernel(tc, xT, w_words, w_scales, b, gate, o
         make_identity(nc, ident[:])
         nc.scalar.activation(warm_out[:], warm[:], ACT.Square)
 
-        nc.sync.dma_start(x[2][:], x_rows[:, 2, :])
+        nc.sync.dma_start(x[0][:], x_rows[:, 0, :])
         nc.sync.dma_start(offs_t[:], offs)
         for q in range(4):
-            nc.sync.dma_start(plane[32 * q + 4:32 * q + 8, S - N:S].bitcast(I32), w_scales[0, 4 * q:4 * q + 4, :].bitcast(I32))
-        for j in (0, 1, 3):
+            nc.sync.dma_start(plane[32 * q + 4:32 * q + 8, 0:N].bitcast(I32), w_scales[0, 4 * q:4 * q + 4, :].bitcast(I32))
+        for j in (1, 2):
             nc.sync.dma_start(x[j][:], x_rows[:, j, :])
+        for h in range(2):
+            nc.sync.dma_start(x[3][:, h * T // 2:(h + 1) * T // 2], x_rows[:, 3, h * T // 2:(h + 1) * T // 2])
         nc.sync.dma_start(w_codes[:], w_words[0].rearrange("p n t -> p (n t)").bitcast(I32))
         with nc.allow_non_contiguous_dma(reason="one bias value to a partition"):
             nc.sync.dma_start(bias[:, :, 0:1], b.rearrange("(c p) o -> p c o", p=P))
@@ -64,62 +66,63 @@ def tile_picked_sub_lin_relu2_sub_e_kernel(tc, xT, w_words, w_scales, b, gate, o
             return offs_t[:, lo // G:hi // G]
 
         H = S // 2
-        W = 192
-        woven = [(0, P), (P, W)]
-        packed = [sb.tile([P, hi - lo, 4], BF16, name=f"packed{lo}", align_bytes=64) for lo, hi in woven]
-        direct = sb.tile([P, S - W, 4], BF16, name="direct", align_bytes=64)
-        rows = sb.tile([P, 4, S], BF16, name="rows", align_bytes=64)
-        x0_rounded = sb.tile([P, T], BF16, name="x0_rounded", align_bytes=64)
+        W = 352
+        woven = sb.tile([P, S, 4], BF16, name="woven", align_bytes=64)
+        rounded = [sb.tile([P, T], BF16, name=f"rounded{j}", tag=f"rounded{j}", align_bytes=64) for j in range(4)]
 
-        nc.vector.tensor_copy(rows[:, 2, 0:W], x[2][:].indirect(picks(0, W)))
-        nc.vector.tensor_copy(direct[:, :, 2], x[2][:].indirect(picks(W, S)))
-        nc.scalar.copy(x0_rounded[:], x[0][:])
-        nc.scalar.activation(rows[:, 0, 0:W], x0_rounded[:].indirect(picks(0, W)), ACT.Copy)
-        nc.vector.tensor_copy(rows[:, 0, W:S], x[0][:].indirect(picks(W, S)))
-        for lo, hi in ((W, S), (0, W)):
-            nc.vector.tensor_copy(rows[:, 1, lo:hi], x[1][:].indirect(picks(lo, hi)))
-        nc.scalar.copy(direct[:, :, 0:2], rows[:, 0:2, W:S].rearrange("p u n -> p n u"))
-        for lo, hi in woven:
-            nc.vector.tensor_copy(rows[:, 3, lo:hi], x[3][:].indirect(picks(lo, hi)))
-        for lo, hi in ((W, 3 * P), (3 * P, S)):
-            nc.vector.tensor_copy(direct[:, lo - W:hi - W, 3], x[3][:].indirect(picks(lo, hi)))
-        for i, (lo, hi) in enumerate(woven):
-            nc.scalar.copy(packed[i][:].rearrange("p (c n) t -> p c t n", n=4), rows[:, :, lo:hi].rearrange("p t (c n) -> p c t n", n=4))
+        def round_on_gpsimd(j, lo, hi):
+            nc.gpsimd.tensor_scalar(rounded[j][:, lo:hi], x[j][:, lo:hi], 1.0, 0.0, ALU.mult, ALU.add)
+
+        def place_on_scalar(j):
+            nc.scalar.activation(woven[:, W:S, j], rounded[j][:].indirect(picks(W, S)), ACT.Copy)
+
+        for j, C in enumerate((640, 384, 544)):
+            nc.vector.tensor_copy(woven[:, 0:W, j], x[j][:].indirect(picks(0, W)))
+            nc.scalar.copy(rounded[j][:, 0:C], x[j][:, 0:C])
+            round_on_gpsimd(j, C, T)
+            if j < 2:
+                place_on_scalar(j)
+        round_on_gpsimd(3, 0, T // 2)
+        round_on_gpsimd(3, T // 2, 768)
+        nc.scalar.copy(rounded[3][:, 768:T], x[3][:, 768:T])
+        place_on_scalar(2)
+        place_on_scalar(3)
+        for lo, hi in ((0, P), (P, W)):
+            nc.vector.tensor_copy(woven[:, lo:hi, 3], x[3][:].indirect(picks(lo, hi)))
 
         codes = sb.tile([P, S], U32, name="codes", align_bytes=64)
-        pieces = [(slice(H, 3 * P), direct[:, H - W:3 * P - W, :]), (slice(W, H), direct[:, 0:H - W, :]), (slice(0, P), packed[0][:]),
-                  (slice(3 * P, S), direct[:, 3 * P - W:S - W, :]), (slice(P, W), packed[1][:])]
-        for cols, source in pieces:
-            nc.vector.quantize_mx(out=codes[:, cols].bitcast(FP8X4), scales=plane[:, cols], in_=source.rearrange("p n j -> p (n j)"))
+        for lo, hi in ((0, 128), (128, 256), (256, 320), (384, S), (320, 384)):
+            source = woven[:, lo:hi, :]
+            nc.vector.quantize_mx(out=codes[:, lo:hi].bitcast(FP8X4), scales=plane[:, lo:hi], in_=source.rearrange("p n j -> p (n j)"))
 
         def product(acc, c, cols):
             nc.tensor.matmul_mx(
                 out=acc,
                 lhsT=w_codes[:, c * P:(c + 1) * P].bitcast(FP8X4),
-                lhsT_scale=plane[4:P, S - N + c * P:S - N + (c + 1) * P],
+                lhsT_scale=plane[4:P, c * P:(c + 1) * P],
                 rhs=codes[:, cols].bitcast(FP8X4),
                 rhs_scale=plane[:, cols],
                 start=True,
                 stop=True,
             )
 
-        spans = [slice(i * P, (i + 1) * P) for i in (2, 0, 3, 1)]
+        spans = [slice(i * P, (i + 1) * P) for i in (0, 1, 3, 2)]
         acc0 = []
         for i, cols in enumerate(spans):
             acc0.append(psum.tile([P, cols.stop - cols.start], F32, name=f"acc0_{i}", tag=f"acc0_{i}"))
             product(acc0[i][:], 0, cols)
-        acc1 = [psum.tile([P, H], F32, name="acc1_0")]
-        product(acc1[0][:], 1, slice(0, H))
 
-        r = [sb.tile([P, S], F32, name=f"r{c}", align_bytes=64) for c in range(2)]
+        r = [sb.tile([P, S], F32, name=f"r{c}", tag=("rounded3", "r1")[c], align_bytes=64) for c in range(2)]
         y = [sb.tile([P, S], F32, name=f"y{c}", align_bytes=64) for c in range(2)]
         for i in (0, 1, 2):
             nc.scalar.activation(r[0][:, spans[i]], acc0[i][:], ACT.Relu, bias=bias[:, 0, 0:1])
+        acc1 = [psum.tile([P, H], F32, name="acc1_0", tag="acc0_0")]
+        product(acc1[0][:], 1, slice(0, H))
         for i in (0, 1, 2):
             nc.scalar.activation(y[0][:, spans[i]], r[0][:, spans[i]], ACT.Square)
         for i in (3,):
             nc.vector.tensor_scalar(r[0][:, spans[i]], acc0[i][:], bias[:, 0, 0:1], 0.0, ALU.add, ALU.max)
-        nc.scalar.activation(y[0][:, P:H], r[0][:, P:H], ACT.Square)
+        nc.scalar.activation(y[0][:, spans[3]], r[0][:, spans[3]], ACT.Square)
         acc1.append(psum.tile([P, H], F32, name="acc1_1", tag="acc0_3"))
         product(acc1[1][:], 1, slice(H, S))
         for h in range(2):

@@ -66,7 +66,7 @@ def tile_picked_sub_lin_relu2_sub_e_kernel(tc, xT, w_words, w_scales, b, gate, o
             return offs_t[:, lo // G:hi // G]
 
         H = S // 2
-        W = 352
+        W = (352, 352, 384, 384)
         woven = sb.tile([P, S, 4], BF16, name="woven", align_bytes=64)
         rounded = [sb.tile([P, T], BF16, name=f"rounded{j}", tag=f"rounded{j}", align_bytes=64) for j in range(4)]
 
@@ -74,10 +74,10 @@ def tile_picked_sub_lin_relu2_sub_e_kernel(tc, xT, w_words, w_scales, b, gate, o
             nc.gpsimd.tensor_scalar(rounded[j][:, lo:hi], x[j][:, lo:hi], 1.0, 0.0, ALU.mult, ALU.add)
 
         def place_on_scalar(j):
-            nc.scalar.activation(woven[:, W:S, j], rounded[j][:].indirect(picks(W, S)), ACT.Copy)
+            nc.scalar.activation(woven[:, W[j]:S, j], rounded[j][:].indirect(picks(W[j], S)), ACT.Copy)
 
         for j, C in enumerate((640, 384, 544)):
-            nc.vector.tensor_copy(woven[:, 0:W, j], x[j][:].indirect(picks(0, W)))
+            nc.vector.tensor_copy(woven[:, 0:W[j], j], x[j][:].indirect(picks(0, W[j])))
             nc.scalar.copy(rounded[j][:, 0:C], x[j][:, 0:C])
             round_on_gpsimd(j, C, T)
             if j < 2:
@@ -87,11 +87,11 @@ def tile_picked_sub_lin_relu2_sub_e_kernel(tc, xT, w_words, w_scales, b, gate, o
         nc.scalar.copy(rounded[3][:, 768:T], x[3][:, 768:T])
         place_on_scalar(2)
         place_on_scalar(3)
-        for lo, hi in ((0, P), (P, W)):
+        for lo, hi in ((0, P), (P, W[3])):
             nc.vector.tensor_copy(woven[:, lo:hi, 3], x[3][:].indirect(picks(lo, hi)))
 
         codes = sb.tile([P, S], U32, name="codes", align_bytes=64)
-        for lo, hi in ((0, 128), (128, 256), (256, 320), (384, S), (320, 384)):
+        for lo, hi in ((0, 128), (128, 256), (256, 384), (384, S)):
             source = woven[:, lo:hi, :]
             nc.vector.quantize_mx(out=codes[:, lo:hi].bitcast(FP8X4), scales=plane[:, lo:hi], in_=source.rearrange("p n j -> p (n j)"))
 
@@ -106,7 +106,7 @@ def tile_picked_sub_lin_relu2_sub_e_kernel(tc, xT, w_words, w_scales, b, gate, o
                 stop=True,
             )
 
-        spans = [slice(i * P, (i + 1) * P) for i in (0, 1, 3, 2)]
+        spans = [slice(i * P, (i + 1) * P) for i in (0, 1, 2, 3)]
         acc0 = []
         for i, cols in enumerate(spans):
             acc0.append(psum.tile([P, cols.stop - cols.start], F32, name=f"acc0_{i}", tag=f"acc0_{i}"))

@@ -39,19 +39,17 @@ def tile_picked_sub_lin_relu2_sub_e_kernel(tc, xT, w_words, w_scales, b, gate, o
         warm = sb.tile([P, 8], F32, name="warm")
         warm_out = sb.tile([P, 8], F32, name="warm_out")
 
-        ident = sb.tile([P, P], F32, name="ident", align_bytes=64)
-        nc.vector.memset(warm[:], 0.0)
-        make_identity(nc, ident[:])
-        nc.scalar.activation(warm_out[:], warm[:], ACT.Square)
 
         nc.sync.dma_start(x[0][:], x_rows[:, 0, :])
         nc.sync.dma_start(offs_t[:], offs)
         for q in range(4):
-            nc.sync.dma_start(plane[32 * q + 4:32 * q + 8, 0:N].bitcast(I32), w_scales[0, 4 * q:4 * q + 4, :].bitcast(I32))
-        for j in (1, 2):
+            nc.scalar.dma_start(plane[32 * q + 4:32 * q + 8, 0:N].bitcast(I32), w_scales[0, 4 * q:4 * q + 4, :].bitcast(I32))
+        ident = sb.tile([P, P], F32, name="ident", align_bytes=64)
+        nc.vector.memset(warm[:], 0.0)
+        make_identity(nc, ident[:])
+        nc.scalar.activation(warm_out[:], warm[:], ACT.Square)
+        for j in (1, 2, 3):
             nc.sync.dma_start(x[j][:], x_rows[:, j, :])
-        for h in range(2):
-            nc.sync.dma_start(x[3][:, h * T // 2:(h + 1) * T // 2], x_rows[:, 3, h * T // 2:(h + 1) * T // 2])
         nc.sync.dma_start(w_codes[:], w_words[0].rearrange("p n t -> p (n t)").bitcast(I32))
         with nc.allow_non_contiguous_dma(reason="one bias value to a partition"):
             nc.sync.dma_start(bias[:, :, 0:1], b.rearrange("(c p) o -> p c o", p=P))
@@ -68,7 +66,7 @@ def tile_picked_sub_lin_relu2_sub_e_kernel(tc, xT, w_words, w_scales, b, gate, o
         H = S // 2
         W = (352, 352, 384, 384)
         woven = sb.tile([P, S, 4], BF16, name="woven", align_bytes=64)
-        rounded = [sb.tile([P, T], BF16, name=f"rounded{j}", tag=f"rounded{j}", align_bytes=64) for j in range(4)]
+        rounded = [sb.tile([P, T], BF16, name=f"rounded{j}", tag=f"rounded{j % 2}", align_bytes=64) for j in range(4)]
 
         def round_on_gpsimd(j, lo, hi):
             nc.gpsimd.tensor_scalar(rounded[j][:, lo:hi], x[j][:, lo:hi], 1.0, 0.0, ALU.mult, ALU.add)
@@ -76,15 +74,14 @@ def tile_picked_sub_lin_relu2_sub_e_kernel(tc, xT, w_words, w_scales, b, gate, o
         def place_on_scalar(j):
             nc.scalar.activation(woven[:, W[j]:S, j], rounded[j][:].indirect(picks(W[j], S)), ACT.Copy)
 
-        for j, C in enumerate((640, 384, 544)):
+        for j, C in enumerate((640, 384, 256)):
             nc.vector.tensor_copy(woven[:, 0:W[j], j], x[j][:].indirect(picks(0, W[j])))
             nc.scalar.copy(rounded[j][:, 0:C], x[j][:, 0:C])
             round_on_gpsimd(j, C, T)
             if j < 2:
                 place_on_scalar(j)
-        round_on_gpsimd(3, 0, T // 2)
-        round_on_gpsimd(3, T // 2, 768)
-        nc.scalar.copy(rounded[3][:, 768:T], x[3][:, 768:T])
+        nc.scalar.copy(rounded[3][:, 0:448], x[3][:, 0:448])
+        round_on_gpsimd(3, 448, T)
         place_on_scalar(2)
         place_on_scalar(3)
         for lo, hi in ((0, P), (P, W[3])):
@@ -112,7 +109,7 @@ def tile_picked_sub_lin_relu2_sub_e_kernel(tc, xT, w_words, w_scales, b, gate, o
             acc0.append(psum.tile([P, cols.stop - cols.start], F32, name=f"acc0_{i}", tag=f"acc0_{i}"))
             product(acc0[i][:], 0, cols)
 
-        r = [sb.tile([P, S], F32, name=f"r{c}", tag=("rounded3", "r1")[c], align_bytes=64) for c in range(2)]
+        r = [sb.tile([P, S], F32, name=f"r{c}", tag=("rounded1", "r1")[c], align_bytes=64) for c in range(2)]
         y = [sb.tile([P, S], F32, name=f"y{c}", align_bytes=64) for c in range(2)]
         for i in (0, 1, 2):
             nc.scalar.activation(r[0][:, spans[i]], acc0[i][:], ACT.Relu, bias=bias[:, 0, 0:1])

@@ -36,18 +36,14 @@ def tile_picked_sub_lin_relu2_sub_e_kernel(tc, xT, w_words, w_scales, b, gate, o
         bias = sb.tile([P, 2, 8], F32, name="bias")
         gates = sb.tile([P, D, V], F32, name="gates", align_bytes=64)
         gate_col = sb.tile([P, 2, 8], F32, name="gate_col")
-        warm = sb.tile([P, 8], F32, name="warm")
-        warm_out = sb.tile([P, 8], F32, name="warm_out")
 
 
-        nc.sync.dma_start(x[0][:], x_rows[:, 0, :])
         nc.sync.dma_start(offs_t[:], offs)
+        nc.sync.dma_start(x[0][:], x_rows[:, 0, :])
         for q in range(4):
-            nc.scalar.dma_start(plane[32 * q + 4:32 * q + 8, 0:N].bitcast(I32), w_scales[0, 4 * q:4 * q + 4, :].bitcast(I32))
+            nc.scalar.dma_start(plane[32 * q + 4:32 * q + 8, P:P + N].bitcast(I32), w_scales[0, 4 * q:4 * q + 4, :].bitcast(I32))
         ident = sb.tile([P, P], F32, name="ident", align_bytes=64)
-        nc.vector.memset(warm[:], 0.0)
         make_identity(nc, ident[:])
-        nc.scalar.activation(warm_out[:], warm[:], ACT.Square)
         for j in (1, 2, 3):
             nc.sync.dma_start(x[j][:], x_rows[:, j, :])
         nc.sync.dma_start(w_codes[:], w_words[0].rearrange("p n t -> p (n t)").bitcast(I32))
@@ -84,11 +80,11 @@ def tile_picked_sub_lin_relu2_sub_e_kernel(tc, xT, w_words, w_scales, b, gate, o
         round_on_gpsimd(3, 448, T)
         place_on_scalar(2)
         place_on_scalar(3)
-        for lo, hi in ((0, P), (P, W[3])):
+        for lo, hi in ((P, W[3]), (0, P)):
             nc.vector.tensor_copy(woven[:, lo:hi, 3], x[3][:].indirect(picks(lo, hi)))
 
         codes = sb.tile([P, S], U32, name="codes", align_bytes=64)
-        for lo, hi in ((0, 128), (128, 256), (256, 384), (384, S)):
+        for lo, hi in ((128, 256), (256, 384), (0, 128), (384, S)):
             source = woven[:, lo:hi, :]
             nc.vector.quantize_mx(out=codes[:, lo:hi].bitcast(FP8X4), scales=plane[:, lo:hi], in_=source.rearrange("p n j -> p (n j)"))
 
@@ -96,14 +92,14 @@ def tile_picked_sub_lin_relu2_sub_e_kernel(tc, xT, w_words, w_scales, b, gate, o
             nc.tensor.matmul_mx(
                 out=acc,
                 lhsT=w_codes[:, c * P:(c + 1) * P].bitcast(FP8X4),
-                lhsT_scale=plane[4:P, c * P:(c + 1) * P],
+                lhsT_scale=plane[4:P, (c + 1) * P:(c + 2) * P],
                 rhs=codes[:, cols].bitcast(FP8X4),
                 rhs_scale=plane[:, cols],
                 start=True,
                 stop=True,
             )
 
-        spans = [slice(i * P, (i + 1) * P) for i in (0, 1, 2, 3)]
+        spans = [slice(i * P, (i + 1) * P) for i in (1, 2, 0, 3)]
         acc0 = []
         for i, cols in enumerate(spans):
             acc0.append(psum.tile([P, cols.stop - cols.start], F32, name=f"acc0_{i}", tag=f"acc0_{i}"))

@@ -38,8 +38,8 @@ def tile_picked_sub_lin_relu2_sub_e_kernel(tc, xT, w_words, w_scales, b, gate, o
         gate_col = sb.tile([P, 2, 8], F32, name="gate_col")
 
 
-        nc.sync.dma_start(offs_t[:], offs)
         nc.sync.dma_start(x[0][:], x_rows[:, 0, :])
+        nc.sync.dma_start(offs_t[:], offs)
         for q in range(4):
             nc.scalar.dma_start(plane[32 * q + 4:32 * q + 8, P:P + N].bitcast(I32), w_scales[0, 4 * q:4 * q + 4, :].bitcast(I32))
         ident = sb.tile([P, P], F32, name="ident", align_bytes=64)
@@ -76,8 +76,8 @@ def tile_picked_sub_lin_relu2_sub_e_kernel(tc, xT, w_words, w_scales, b, gate, o
             round_on_gpsimd(j, C, T)
             if j < 2:
                 place_on_scalar(j)
-        nc.scalar.copy(rounded[3][:, 0:448], x[3][:, 0:448])
-        round_on_gpsimd(3, 448, T)
+        nc.scalar.copy(rounded[3][:, 0:512], x[3][:, 0:512])
+        round_on_gpsimd(3, 512, T)
         place_on_scalar(2)
         place_on_scalar(3)
         for lo, hi in ((P, W[3]), (0, P)):

@@ -60,7 +60,7 @@ def tile_picked_sub_lin_relu2_sub_e_kernel(tc, xT, w_words, w_scales, b, gate, o
             return offs_t[:, lo // G:hi // G]
 
         H = S // 2
-        W = (352, 352, 384, 384)
+        W = (320, 320, 384, 384)
         woven = sb.tile([P, S, 4], BF16, name="woven", align_bytes=64)
         rounded = [sb.tile([P, T], BF16, name=f"rounded{j}", tag=f"rounded{j % 2}", align_bytes=64) for j in range(4)]
 
@@ -70,7 +70,7 @@ def tile_picked_sub_lin_relu2_sub_e_kernel(tc, xT, w_words, w_scales, b, gate, o
         def place_on_scalar(j):
             nc.scalar.activation(woven[:, W[j]:S, j], rounded[j][:].indirect(picks(W[j], S)), ACT.Copy)
 
-        for j, C in enumerate((640, 384, 256)):
+        for j, C in enumerate((640, 224, 224)):
             nc.vector.tensor_copy(woven[:, 0:W[j], j], x[j][:].indirect(picks(0, W[j])))
             nc.scalar.copy(rounded[j][:, 0:C], x[j][:, 0:C])
             round_on_gpsimd(j, C, T)

@@ -35,13 +35,13 @@ def tile_picked_sub_lin_relu2_sub_e_kernel(tc, xT, w_words, w_scales, b, gate, o
         plane = sb.tile([P, S], U8, name="plane", align_bytes=64)
         bias = sb.tile([P, 2, 8], F32, name="bias")
         gates = sb.tile([P, D, V], F32, name="gates", align_bytes=64)
-        gate_col = sb.tile([P, 2, 8], F32, name="gate_col")
-
+        gate_col = sb.tile([P, 2, 2, 8], F32, name="gate_col")
 
         nc.sync.dma_start(x[0][:], x_rows[:, 0, :])
         nc.sync.dma_start(offs_t[:], offs)
         for q in range(4):
-            nc.scalar.dma_start(plane[32 * q + 4:32 * q + 8, P:P + N].bitcast(I32), w_scales[0, 4 * q:4 * q + 4, :].bitcast(I32))
+            rows = w_scales[0, 4 * q:4 * q + 4, :].bitcast(I32).rearrange("r (c m) -> c r m", c=2)
+            nc.scalar.dma_start(plane[32 * q + 4:32 * q + 12, 0:P].bitcast(I32), rows)
         ident = sb.tile([P, P], F32, name="ident", align_bytes=64)
         make_identity(nc, ident[:])
         for j in (1, 2, 3):
@@ -54,15 +54,17 @@ def tile_picked_sub_lin_relu2_sub_e_kernel(tc, xT, w_words, w_scales, b, gate, o
         nc.sync.dma_start(pos_t[2][:], pos3)
         nc.sync.dma_start(gates[:], gate[:, 0:P, :].rearrange("d p v -> p d v"))
         with nc.allow_non_contiguous_dma(reason="one gate value to a partition"):
-            nc.sync.dma_start(gate_col[:, :, 0:1], gate[0, 0:1, :].rearrange("o (h p) -> p h o", p=P))
+            for d in range(2):
+                nc.sync.dma_start(gate_col[:, d, :, 0:1], gate[d, 0:1, :].rearrange("o (h p) -> p h o", p=P))
 
         def picks(lo, hi):
             return offs_t[:, lo // G:hi // G]
 
-        H = S // 2
         W = (320, 320, 384, 384)
         woven = sb.tile([P, S, 4], BF16, name="woven", align_bytes=64)
         rounded = [sb.tile([P, T], BF16, name=f"rounded{j}", tag=f"rounded{j % 2}", align_bytes=64) for j in range(4)]
+        codes = sb.tile([P, S], U32, name="codes", align_bytes=64)
+        pieces = [slice(i * P, (i + 1) * P) for i in range(4)]
 
         def round_on_gpsimd(j, lo, hi):
             nc.gpsimd.tensor_scalar(rounded[j][:, lo:hi], x[j][:, lo:hi], 1.0, 0.0, ALU.mult, ALU.add)
@@ -70,8 +72,28 @@ def tile_picked_sub_lin_relu2_sub_e_kernel(tc, xT, w_words, w_scales, b, gate, o
         def place_on_scalar(j):
             nc.scalar.activation(woven[:, W[j]:S, j], rounded[j][:].indirect(picks(W[j], S)), ACT.Copy)
 
+        def place_on_vector(j, lo, hi):
+            nc.vector.tensor_copy(woven[:, lo:hi, j], x[j][:].indirect(picks(lo, hi)))
+
+        def quantise(i):
+            source = woven[:, pieces[i], :].rearrange("p n j -> p (n j)")
+            nc.vector.quantize_mx(out=codes[:, pieces[i]].bitcast(FP8X4), scales=plane[:, pieces[i]], in_=source)
+
+        acc = [[psum.tile([P, P], F32, name=f"acc{c}_{i}", tag=f"bank{c}_{i}") for i in range(4)] for c in range(2)]
+
+        def product(c, i):
+            nc.tensor.matmul_mx(
+                out=acc[c][i][:],
+                lhsT=w_codes[:, c * P:(c + 1) * P].bitcast(FP8X4),
+                lhsT_scale=plane[4 + 4 * c:P, 0:P],
+                rhs=codes[:, pieces[i]].bitcast(FP8X4),
+                rhs_scale=plane[:, pieces[i]],
+                start=True,
+                stop=True,
+            )
+
         for j, C in enumerate((640, 224, 224)):
-            nc.vector.tensor_copy(woven[:, 0:W[j], j], x[j][:].indirect(picks(0, W[j])))
+            place_on_vector(j, 0, W[j])
             nc.scalar.copy(rounded[j][:, 0:C], x[j][:, 0:C])
             round_on_gpsimd(j, C, T)
             if j < 2:
@@ -80,86 +102,72 @@ def tile_picked_sub_lin_relu2_sub_e_kernel(tc, xT, w_words, w_scales, b, gate, o
         round_on_gpsimd(3, 512, T)
         place_on_scalar(2)
         place_on_scalar(3)
-        for lo, hi in ((P, W[3]), (0, P)):
-            nc.vector.tensor_copy(woven[:, lo:hi, 3], x[3][:].indirect(picks(lo, hi)))
+        place_on_vector(3, 0, P)
+        place_on_vector(3, P, 2 * P)
+        quantise(0)
+        place_on_vector(3, 2 * P, 3 * P)
+        for i in (1, 2, 3):
+            quantise(i)
+        for i in range(4):
+            product(0, i)
+            product(1, i)
 
-        codes = sb.tile([P, S], U32, name="codes", align_bytes=64)
-        for lo, hi in ((128, 256), (256, 384), (0, 128), (384, S)):
-            source = woven[:, lo:hi, :]
-            nc.vector.quantize_mx(out=codes[:, lo:hi].bitcast(FP8X4), scales=plane[:, lo:hi], in_=source.rearrange("p n j -> p (n j)"))
-
-        def product(acc, c, cols):
-            nc.tensor.matmul_mx(
-                out=acc,
-                lhsT=w_codes[:, c * P:(c + 1) * P].bitcast(FP8X4),
-                lhsT_scale=plane[4:P, (c + 1) * P:(c + 2) * P],
-                rhs=codes[:, cols].bitcast(FP8X4),
-                rhs_scale=plane[:, cols],
-                start=True,
-                stop=True,
-            )
-
-        spans = [slice(i * P, (i + 1) * P) for i in (1, 2, 0, 3)]
-        acc0 = []
-        for i, cols in enumerate(spans):
-            acc0.append(psum.tile([P, cols.stop - cols.start], F32, name=f"acc0_{i}", tag=f"acc0_{i}"))
-            product(acc0[i][:], 0, cols)
-
-        r = [sb.tile([P, S], F32, name=f"r{c}", tag=("rounded1", "r1")[c], align_bytes=64) for c in range(2)]
+        r = [sb.tile([P, S], F32, name=f"r{c}", tag=("rounded1", "woven")[c], align_bytes=64) for c in range(2)]
         y = [sb.tile([P, S], F32, name=f"y{c}", align_bytes=64) for c in range(2)]
-        for i in (0, 1, 2):
-            nc.scalar.activation(r[0][:, spans[i]], acc0[i][:], ACT.Relu, bias=bias[:, 0, 0:1])
-        acc1 = [psum.tile([P, H], F32, name="acc1_0", tag="acc0_0")]
-        product(acc1[0][:], 1, slice(0, H))
-        for i in (0, 1, 2):
-            nc.scalar.activation(y[0][:, spans[i]], r[0][:, spans[i]], ACT.Square)
-        for i in (3,):
-            nc.vector.tensor_scalar(r[0][:, spans[i]], acc0[i][:], bias[:, 0, 0:1], 0.0, ALU.add, ALU.max)
-        nc.scalar.activation(y[0][:, spans[3]], r[0][:, spans[3]], ACT.Square)
-        acc1.append(psum.tile([P, H], F32, name="acc1_1", tag="acc0_3"))
-        product(acc1[1][:], 1, slice(H, S))
-        for h in range(2):
-            nc.scalar.activation(r[1][:, h * H:(h + 1) * H], acc1[h][:], ACT.Relu, bias=bias[:, 1, 0:1])
-        for h in range(2):
-            nc.scalar.activation(y[1][:, h * H:(h + 1) * H], r[1][:, h * H:(h + 1) * H], ACT.Square)
+        for i in range(4):
+            nc.scalar.activation(r[0][:, pieces[i]], acc[0][i][:], ACT.Relu, bias=bias[:, 0, 0:1])
+            nc.vector.tensor_scalar(r[1][:, pieces[i]], acc[1][i][:], bias[:, 1, 0:1], 0.0, ALU.add, ALU.max)
+        for i in range(4):
+            nc.scalar.activation(y[0][:, pieces[i]], r[0][:, pieces[i]], ACT.Square)
+            nc.vector.tensor_tensor(y[1][:, pieces[i]], r[1][:, pieces[i]], r[1][:, pieces[i]], ALU.mult)
 
-        terms = [sb.tile([P, D, V], F32, name=f"terms{c}", align_bytes=64) for c in range(2)]
+        terms = [sb.tile([P, D, V], F32, name=f"terms{c}", tag=("terms0", "rounded1")[c], align_bytes=64) for c in range(2)]
         part = sb.tile([P, V], F32, name="part", align_bytes=64)
         res = [sb.tile([P, V], F32, name=f"res{c}", align_bytes=64) for c in range(2)]
 
-        def fetch(c, d, lo, hi):
-            nc.vector.tensor_tensor(terms[c][:, d, lo:hi], y[c][:].indirect(pos_t[d][:, lo // G:hi // G]), gates[:, d, lo:hi], ALU.mult)
+        def entries(d, lo, hi):
+            return pos_t[d][:, lo // G:hi // G]
 
-        unsquared = sb.tile([P, V], F32, name="unsquared", align_bytes=64)
-        turned_sb = sb.tile([P, 2, 2, P], F32, name="turned_sb", align_bytes=64)
-        first = psum.tile([P, 2, P], F32, name="first", tag="acc0_0")
-        turned = [psum.tile([P, P], F32, name=f"turned{h}", tag=f"turned{h}") for h in range(2)]
-        back = [psum.tile([P, P], F32, name=f"back{h}", tag=f"acc0_{1 + h}") for h in range(2)]
-        nc.vector.tensor_copy(unsquared[:], r[0][:].indirect(pos_t[0][:]))
-        nc.scalar.activation(terms[0][:, 0, :], unsquared[:], ACT.Square)
-        for h in range(2):
-            nc.tensor.transpose(first[:, h, :], terms[0][:, 0, h * P:(h + 1) * P], ident[:])
-        for h in range(2):
-            nc.scalar.activation(turned_sb[:, 0, h, :], first[:, h, :], ACT.Copy, scale=gate_col[:, h, 0:1])
-        for d in (1, 2):
-            fetch(0, d, 0, V)
-            for h in range(2):
-                nc.tensor.matmul(turned[h][:], terms[0][:, d, h * P:(h + 1) * P], ident[:], start=(d == 1), stop=(d == 2), is_transpose=True)
-        for h in range(2):
-            nc.scalar.copy(turned_sb[:, 1, h, :], turned[h][:])
-        for h in range(2):
-            for e in range(2):
-                nc.tensor.matmul(back[h][:], turned_sb[:, e, h, :], ident[:], start=(e == 0), stop=(e == 1), is_transpose=True)
-        for h in range(2):
-            cols = slice(h * P, (h + 1) * P)
-            nc.scalar.copy(res[0][:, cols], back[h][:])
-            nc.scalar.dma_start(out[0:P, cols], res[0][:, cols])
+        def fetch_weighted(c, d, lo, hi):
+            nc.vector.tensor_tensor(terms[c][:, d, lo:hi], y[c][:].indirect(entries(d, lo, hi)), gates[:, d, lo:hi], ALU.mult)
 
-        fetch(1, 0, 0, V)
-        fetch(1, 1, 0, V)
-        fetch(1, 2, 0, 192)
+        def fetch_plain(d, lo, hi):
+            nc.scalar.activation(terms[0][:, d, lo:hi], y[0][:].indirect(entries(d, lo, hi)), ACT.Copy)
+
+        halves = [slice(h * P, (h + 1) * P) for h in range(2)]
+        turned_sb = sb.tile([P, D, 2, P], F32, name="turned_sb", align_bytes=64)
+        turned0 = psum.tile([P, 2, P], F32, name="turned0", tag="bank0_0")
+        turned2 = psum.tile([P, 2, P], F32, name="turned2", tag="bank0_1")
+        turned1 = [psum.tile([P, P], F32, name=f"turned1_{h}", tag=f"bank0_{2 + h}") for h in range(2)]
+        back = [psum.tile([P, P], F32, name=f"back{h}", tag=f"bank1_{h}") for h in range(2)]
+
+        fetch_plain(0, 0, V)
+        fetch_weighted(0, 2, 0, V)
+        for h in range(2):
+            fetch_plain(1, h * P, (h + 1) * P)
+        for h in range(2):
+            nc.tensor.transpose(turned0[:, h, :], terms[0][:, 0, halves[h]], ident[:])
+        for h in range(2):
+            nc.tensor.transpose(turned2[:, h, :], terms[0][:, 2, halves[h]], ident[:])
+        for h in range(2):
+            nc.tensor.transpose(turned1[h][:], terms[0][:, 1, halves[h]], ident[:])
+        for h in range(2):
+            nc.scalar.activation(turned_sb[:, 0, h, :], turned0[:, h, :], ACT.Copy, scale=gate_col[:, 0, h, 0:1])
+        nc.scalar.copy(turned_sb[:, 2, :, :], turned2[:])
+        for h in range(2):
+            nc.scalar.activation(turned_sb[:, 1, h, :], turned1[h][:], ACT.Copy, scale=gate_col[:, 1, h, 0:1])
+        for h in range(2):
+            for e, d in enumerate((0, 2, 1)):
+                nc.tensor.matmul(back[h][:], turned_sb[:, d, h, :], ident[:], start=(e == 0), stop=(e == 2), is_transpose=True)
+        for h in range(2):
+            nc.scalar.copy(res[0][:, halves[h]], back[h][:])
+            nc.scalar.dma_start(out[0:P, halves[h]], res[0][:, halves[h]])
+
+        fetch_weighted(1, 0, 0, V)
+        fetch_weighted(1, 1, 0, V)
+        fetch_weighted(1, 2, 0, 192)
         nc.vector.tensor_tensor(part[:], terms[1][:, 0, :], terms[1][:, 1, :], ALU.add)
-        fetch(1, 2, 192, V)
+        fetch_weighted(1, 2, 192, V)
         for lo, hi in ((0, 192), (192, V)):
             nc.vector.tensor_tensor(res[1][:, lo:hi], part[:, lo:hi], terms[1][:, 2, lo:hi], ALU.add)
             nc.sync.dma_start(out[P:N, lo:hi], res[1][:, lo:hi])

@@ -40,8 +40,7 @@ def tile_picked_sub_lin_relu2_sub_e_kernel(tc, xT, w_words, w_scales, b, gate, o
         nc.sync.dma_start(x[0][:], x_rows[:, 0, :])
         nc.sync.dma_start(offs_t[:], offs)
         for q in range(4):
-            rows = w_scales[0, 4 * q:4 * q + 4, :].bitcast(I32).rearrange("r (c m) -> c r m", c=2)
-            nc.scalar.dma_start(plane[32 * q + 4:32 * q + 12, 0:P].bitcast(I32), rows)
+            nc.scalar.dma_start(plane[32 * q + 4:32 * q + 8, 0:N].bitcast(I32), w_scales[0, 4 * q:4 * q + 4, :].bitcast(I32))
         ident = sb.tile([P, P], F32, name="ident", align_bytes=64)
         make_identity(nc, ident[:])
         for j in (1, 2, 3):
@@ -85,7 +84,7 @@ def tile_picked_sub_lin_relu2_sub_e_kernel(tc, xT, w_words, w_scales, b, gate, o
             nc.tensor.matmul_mx(
                 out=acc[c][i][:],
                 lhsT=w_codes[:, c * P:(c + 1) * P].bitcast(FP8X4),
-                lhsT_scale=plane[4 + 4 * c:P, 0:P],
+                lhsT_scale=plane[4:P, c * P:(c + 1) * P],
                 rhs=codes[:, pieces[i]].bitcast(FP8X4),
                 rhs_scale=plane[:, pieces[i]],
                 start=True,
@@ -108,9 +107,8 @@ def tile_picked_sub_lin_relu2_sub_e_kernel(tc, xT, w_words, w_scales, b, gate, o
         place_on_vector(3, 2 * P, 3 * P)
         for i in (1, 2, 3):
             quantise(i)
-        for i in range(4):
-            product(0, i)
-            product(1, i)
+        for c, i in ((0, 0), (0, 1), (1, 0), (1, 1), (0, 2), (0, 3), (1, 2), (1, 3)):
+            product(c, i)
 
         r = [sb.tile([P, S], F32, name=f"r{c}", tag=("rounded1", "woven")[c], align_bytes=64) for c in range(2)]
         y = [sb.tile([P, S], F32, name=f"y{c}", align_bytes=64) for c in range(2)]

@@ -53,8 +53,8 @@ def tile_picked_sub_lin_relu2_sub_e_kernel(tc, xT, w_words, w_scales, b, gate, o
         nc.sync.dma_start(pos_t[2][:], pos3)
         nc.sync.dma_start(gates[:], gate[:, 0:P, :].rearrange("d p v -> p d v"))
         with nc.allow_non_contiguous_dma(reason="one gate value to a partition"):
-            for d in range(2):
-                nc.sync.dma_start(gate_col[:, d, :, 0:1], gate[d, 0:1, :].rearrange("o (h p) -> p h o", p=P))
+            nc.sync.dma_start(gate_col[:, 0, :, 0:1], gate[0, 0:1, :].rearrange("o (h p) -> p h o", p=P))
+            nc.sync.dma_start(gate_col[:, 1, 0, 0:1], gate[1, 0:1, 0:P].rearrange("o p -> p o"))
 
         def picks(lo, hi):
             return offs_t[:, lo // G:hi // G]
@@ -133,33 +133,31 @@ def tile_picked_sub_lin_relu2_sub_e_kernel(tc, xT, w_words, w_scales, b, gate, o
             nc.scalar.activation(terms[0][:, d, lo:hi], y[0][:].indirect(entries(d, lo, hi)), ACT.Copy)
 
         halves = [slice(h * P, (h + 1) * P) for h in range(2)]
-        turned_sb = sb.tile([P, D, 2, P], F32, name="turned_sb", align_bytes=64)
-        turned0 = psum.tile([P, 2, P], F32, name="turned0", tag="bank0_0")
-        turned2 = psum.tile([P, 2, P], F32, name="turned2", tag="bank0_1")
-        turned1 = [psum.tile([P, P], F32, name=f"turned1_{h}", tag=f"bank0_{2 + h}") for h in range(2)]
-        back = [psum.tile([P, P], F32, name=f"back{h}", tag=f"bank1_{h}") for h in range(2)]
+        steps = ((0, 0), (2, 0), (0, 1), (2, 1), (1, 0))
+        banks = ("bank0_0", "bank0_1", "bank0_2", "bank0_3", "bank1_0")
+        turned = {step: psum.tile([P, P], F32, name=f"turned{step[0]}_{step[1]}", tag=tag) for step, tag in zip(steps, banks)}
+        turned_sb = {step: sb.tile([P, P], F32, name=f"turned_sb{step[0]}_{step[1]}", align_bytes=64) for step in steps}
+        back = [psum.tile([P, P], F32, name=f"back{h}", tag=f"bank1_{1 + h}") for h in range(2)]
 
-        fetch_plain(0, 0, V)
+        fetch_plain(0, 0, P)
         fetch_weighted(0, 2, 0, V)
-        for h in range(2):
-            fetch_plain(1, h * P, (h + 1) * P)
-        for h in range(2):
-            nc.tensor.transpose(turned0[:, h, :], terms[0][:, 0, halves[h]], ident[:])
-        for h in range(2):
-            nc.tensor.transpose(turned2[:, h, :], terms[0][:, 2, halves[h]], ident[:])
-        for h in range(2):
-            nc.tensor.transpose(turned1[h][:], terms[0][:, 1, halves[h]], ident[:])
-        for h in range(2):
-            nc.scalar.activation(turned_sb[:, 0, h, :], turned0[:, h, :], ACT.Copy, scale=gate_col[:, 0, h, 0:1])
-        nc.scalar.copy(turned_sb[:, 2, :, :], turned2[:])
-        for h in range(2):
-            nc.scalar.activation(turned_sb[:, 1, h, :], turned1[h][:], ACT.Copy, scale=gate_col[:, 1, h, 0:1])
-        for h in range(2):
-            for e, d in enumerate((0, 2, 1)):
-                nc.tensor.matmul(back[h][:], turned_sb[:, d, h, :], ident[:], start=(e == 0), stop=(e == 2), is_transpose=True)
-        for h in range(2):
+        fetch_plain(0, P, V)
+        fetch_weighted(0, 1, P, V)
+        fetch_plain(1, 0, P)
+        for d, h in steps:
+            sources = (2, 1) if (d, h) == (2, 1) else (d,)
+            for e in sources:
+                nc.tensor.matmul(turned[d, h][:], terms[0][:, e, halves[h]], ident[:], start=(e == sources[0]), stop=(e == sources[-1]), is_transpose=True)
+        for d, h in steps:
+            if d == 2:
+                nc.scalar.copy(turned_sb[d, h][:], turned[d, h][:])
+            else:
+                nc.scalar.activation(turned_sb[d, h][:], turned[d, h][:], ACT.Copy, scale=gate_col[:, d, h, 0:1])
+        for d, h in steps:
+            nc.tensor.matmul(back[h][:], turned_sb[d, h][:], ident[:], start=(d == 0), stop=((d, h) in ((2, 1), (1, 0))), is_transpose=True)
+        for h in (1, 0):
             nc.scalar.copy(res[0][:, halves[h]], back[h][:])
-            nc.scalar.dma_start(out[0:P, halves[h]], res[0][:, halves[h]])
+        nc.scalar.dma_start(out[0:P, :], res[0][:])
 
         fetch_weighted(1, 0, 0, V)
         fetch_weighted(1, 1, 0, V)

@@ -43,6 +43,9 @@ def tile_picked_sub_lin_relu2_sub_e_kernel(tc, xT, w_words, w_scales, b, gate, o
             nc.scalar.dma_start(plane[32 * q + 4:32 * q + 8, 0:N].bitcast(I32), w_scales[0, 4 * q:4 * q + 4, :].bitcast(I32))
         ident = sb.tile([P, P], F32, name="ident", align_bytes=64)
         make_identity(nc, ident[:])
+        warm = sb.tile([P, 16], F32, name="warm")
+        nc.vector.memset(warm[:, 0:8], 0.0)
+        nc.scalar.activation(warm[:, 8:16], warm[:, 0:8], ACT.Relu)
         for j in (1, 2, 3):
             nc.sync.dma_start(x[j][:], x_rows[:, j, :])
         nc.sync.dma_start(w_codes[:], w_words[0].rearrange("p n t -> p (n t)").bitcast(I32))
@@ -59,17 +62,18 @@ def tile_picked_sub_lin_relu2_sub_e_kernel(tc, xT, w_words, w_scales, b, gate, o
         def picks(lo, hi):
             return offs_t[:, lo // G:hi // G]
 
-        W = (320, 320, 384, 384)
+        W = (352, 256)
         woven = sb.tile([P, S, 4], BF16, name="woven", align_bytes=64)
-        rounded = [sb.tile([P, T], BF16, name=f"rounded{j}", tag=f"rounded{j % 2}", align_bytes=64) for j in range(4)]
+        staged = [sb.tile([P, 2, S - W[u]], BF16, name=f"staged{u}", align_bytes=64) for u in range(2)]
         codes = sb.tile([P, S], U32, name="codes", align_bytes=64)
         pieces = [slice(i * P, (i + 1) * P) for i in range(4)]
 
-        def round_on_gpsimd(j, lo, hi):
-            nc.gpsimd.tensor_scalar(rounded[j][:, lo:hi], x[j][:, lo:hi], 1.0, 0.0, ALU.mult, ALU.add)
+        def stage_on_scalar(j, lo, hi):
+            first = W[j // 2]
+            nc.scalar.activation(staged[j // 2][:, j % 2, lo - first:hi - first], x[j][:].indirect(picks(lo, hi)), ACT.Copy)
 
-        def place_on_scalar(j):
-            nc.scalar.activation(woven[:, W[j]:S, j], rounded[j][:].indirect(picks(W[j], S)), ACT.Copy)
+        def pair(copy, u, lo, hi):
+            copy(woven[:, lo:hi, 2 * u:2 * u + 2], staged[u][:, :, lo - W[u]:hi - W[u]].rearrange("p j n -> p n j"))
 
         def place_on_vector(j, lo, hi):
             nc.vector.tensor_copy(woven[:, lo:hi, j], x[j][:].indirect(picks(lo, hi)))
@@ -91,26 +95,22 @@ def tile_picked_sub_lin_relu2_sub_e_kernel(tc, xT, w_words, w_scales, b, gate, o
                 stop=True,
             )
 
-        for j, C in enumerate((640, 224, 224)):
-            place_on_vector(j, 0, W[j])
-            nc.scalar.copy(rounded[j][:, 0:C], x[j][:, 0:C])
-            round_on_gpsimd(j, C, T)
-            if j < 2:
-                place_on_scalar(j)
-        nc.scalar.copy(rounded[3][:, 0:512], x[3][:, 0:512])
-        round_on_gpsimd(3, 512, T)
-        place_on_scalar(2)
-        place_on_scalar(3)
-        place_on_vector(3, 0, P)
-        place_on_vector(3, P, 2 * P)
-        quantise(0)
-        place_on_vector(3, 2 * P, 3 * P)
-        for i in (1, 2, 3):
+        for j in range(3):
+            place_on_vector(j, 0, W[j // 2])
+            stage_on_scalar(j, W[j // 2], S)
+            if j == 1:
+                pair(nc.scalar.copy, 0, W[0], S)
+        for i in (0, 1):
+            place_on_vector(3, i * P, (i + 1) * P)
+            stage_on_scalar(3, (i + 2) * P, (i + 3) * P)
+        pair(nc.vector.tensor_copy, 1, 2 * P, 3 * P)
+        pair(nc.scalar.copy, 1, 3 * P, S)
+        for i in range(4):
             quantise(i)
-        for c, i in ((0, 0), (0, 1), (1, 0), (1, 1), (0, 2), (0, 3), (1, 2), (1, 3)):
+        for c, i in ((0, 0), (1, 0), (0, 1), (1, 1), (0, 2), (0, 3), (1, 2), (1, 3)):
             product(c, i)
 
-        r = [sb.tile([P, S], F32, name=f"r{c}", tag=("rounded1", "woven")[c], align_bytes=64) for c in range(2)]
+        r = [sb.tile([P, S], F32, name=f"r{c}", tag=("staged1", "woven")[c], align_bytes=64) for c in range(2)]
         y = [sb.tile([P, S], F32, name=f"y{c}", align_bytes=64) for c in range(2)]
         for i in range(4):
             nc.scalar.activation(r[0][:, pieces[i]], acc[0][i][:], ACT.Relu, bias=bias[:, 0, 0:1])
@@ -119,7 +119,7 @@ def tile_picked_sub_lin_relu2_sub_e_kernel(tc, xT, w_words, w_scales, b, gate, o
             nc.scalar.activation(y[0][:, pieces[i]], r[0][:, pieces[i]], ACT.Square)
             nc.vector.tensor_tensor(y[1][:, pieces[i]], r[1][:, pieces[i]], r[1][:, pieces[i]], ALU.mult)
 
-        terms = [sb.tile([P, D, V], F32, name=f"terms{c}", tag=("terms0", "rounded1")[c], align_bytes=64) for c in range(2)]
+        terms = [sb.tile([P, D, V], F32, name=f"terms{c}", tag=("terms0", "staged1")[c], align_bytes=64) for c in range(2)]
         part = sb.tile([P, V], F32, name="part", align_bytes=64)
         res = [sb.tile([P, V], F32, name=f"res{c}", align_bytes=64) for c in range(2)]
 

@@ -42,10 +42,10 @@ def tile_picked_sub_lin_relu2_sub_e_kernel(tc, xT, w_words, w_scales, b, gate, o
         for q in range(4):
             nc.scalar.dma_start(plane[32 * q + 4:32 * q + 8, 0:N].bitcast(I32), w_scales[0, 4 * q:4 * q + 4, :].bitcast(I32))
         ident = sb.tile([P, P], F32, name="ident", align_bytes=64)
-        make_identity(nc, ident[:])
-        warm = sb.tile([P, 16], F32, name="warm")
-        nc.vector.memset(warm[:, 0:8], 0.0)
-        nc.scalar.activation(warm[:, 8:16], warm[:, 0:8], ACT.Relu)
+        zeros = sb.tile([P, P], F32, name="zeros", align_bytes=64)
+        nc.vector.memset(zeros[:], 0.0)
+        nc.scalar.copy(ident[:], zeros[:])
+        make_identity(nc, ident[:], nomemset=True)
         for j in (1, 2, 3):
             nc.sync.dma_start(x[j][:], x_rows[:, j, :])
         nc.sync.dma_start(w_codes[:], w_words[0].rearrange("p n t -> p (n t)").bitcast(I32))
@@ -62,7 +62,7 @@ def tile_picked_sub_lin_relu2_sub_e_kernel(tc, xT, w_words, w_scales, b, gate, o
         def picks(lo, hi):
             return offs_t[:, lo // G:hi // G]
 
-        W = (352, 256)
+        W = (384, 256)
         woven = sb.tile([P, S, 4], BF16, name="woven", align_bytes=64)
         staged = [sb.tile([P, 2, S - W[u]], BF16, name=f"staged{u}", align_bytes=64) for u in range(2)]
         codes = sb.tile([P, S], U32, name="codes", align_bytes=64)
@@ -103,23 +103,23 @@ def tile_picked_sub_lin_relu2_sub_e_kernel(tc, xT, w_words, w_scales, b, gate, o
         for i in (0, 1):
             place_on_vector(3, i * P, (i + 1) * P)
             stage_on_scalar(3, (i + 2) * P, (i + 3) * P)
-        pair(nc.vector.tensor_copy, 1, 2 * P, 3 * P)
-        pair(nc.scalar.copy, 1, 3 * P, S)
-        for i in range(4):
-            quantise(i)
+        pair(nc.scalar.copy, 1, 2 * P, 3 * P)
+        quantise(0)
+        quantise(1)
+        pair(nc.vector.tensor_copy, 1, 3 * P, S)
+        quantise(2)
+        quantise(3)
         for c, i in ((0, 0), (1, 0), (0, 1), (1, 1), (0, 2), (0, 3), (1, 2), (1, 3)):
             product(c, i)
 
-        r = [sb.tile([P, S], F32, name=f"r{c}", tag=("staged1", "woven")[c], align_bytes=64) for c in range(2)]
-        y = [sb.tile([P, S], F32, name=f"y{c}", align_bytes=64) for c in range(2)]
-        for i in range(4):
-            nc.scalar.activation(r[0][:, pieces[i]], acc[0][i][:], ACT.Relu, bias=bias[:, 0, 0:1])
-            nc.vector.tensor_scalar(r[1][:, pieces[i]], acc[1][i][:], bias[:, 1, 0:1], 0.0, ALU.add, ALU.max)
-        for i in range(4):
-            nc.scalar.activation(y[0][:, pieces[i]], r[0][:, pieces[i]], ACT.Square)
-            nc.vector.tensor_tensor(y[1][:, pieces[i]], r[1][:, pieces[i]], r[1][:, pieces[i]], ALU.mult)
+        r = [sb.tile([P, S], F32, name=f"r{c}", tag=("staged1", "r1")[c], align_bytes=64) for c in range(2)]
+        y = [sb.tile([P, S], F32, name=f"y{c}", tag=("woven", "y1")[c], align_bytes=64) for c in range(2)]
+        for c, i in ((0, 0), (1, 0), (0, 1), (1, 1), (0, 2), (0, 3), (1, 2), (1, 3)):
+            nc.scalar.activation(r[c][:, pieces[i]], acc[c][i][:], ACT.Relu, bias=bias[:, c, 0:1])
+        for c, i in ((0, 0), (1, 0), (0, 1), (1, 1), (0, 2), (0, 3), (1, 2), (1, 3)):
+            nc.vector.tensor_tensor(y[c][:, pieces[i]], r[c][:, pieces[i]], r[c][:, pieces[i]], ALU.mult)
 
-        terms = [sb.tile([P, D, V], F32, name=f"terms{c}", tag=("terms0", "staged1")[c], align_bytes=64) for c in range(2)]
+        terms = [sb.tile([P, D, V], F32, name=f"terms{c}", align_bytes=64) for c in range(2)]
         part = sb.tile([P, V], F32, name="part", align_bytes=64)
         res = [sb.tile([P, V], F32, name=f"res{c}", align_bytes=64) for c in range(2)]
 

@@ -35,7 +35,6 @@ def tile_picked_sub_lin_relu2_sub_e_kernel(tc, xT, w_words, w_scales, b, gate, o
         plane = sb.tile([P, S], U8, name="plane", align_bytes=64)
         bias = sb.tile([P, 2, 8], F32, name="bias")
         gates = sb.tile([P, D, V], F32, name="gates", align_bytes=64)
-        gate_col = sb.tile([P, 2, 2, 8], F32, name="gate_col")
 
         nc.sync.dma_start(x[0][:], x_rows[:, 0, :])
         nc.sync.dma_start(offs_t[:], offs)
@@ -51,13 +50,11 @@ def tile_picked_sub_lin_relu2_sub_e_kernel(tc, xT, w_words, w_scales, b, gate, o
         nc.sync.dma_start(w_codes[:], w_words[0].rearrange("p n t -> p (n t)").bitcast(I32))
         with nc.allow_non_contiguous_dma(reason="one bias value to a partition"):
             nc.sync.dma_start(bias[:, :, 0:1], b.rearrange("(c p) o -> p c o", p=P))
+        nc.sync.dma_start(gates[:, :, P:V], gate[:, 0:P, P:V].rearrange("d p v -> p d v"))
         nc.sync.dma_start(pos_t[0][:], pos1)
         nc.sync.dma_start(pos_t[1][:], pos2)
         nc.sync.dma_start(pos_t[2][:], pos3)
-        nc.sync.dma_start(gates[:], gate[:, 0:P, :].rearrange("d p v -> p d v"))
-        with nc.allow_non_contiguous_dma(reason="one gate value to a partition"):
-            nc.sync.dma_start(gate_col[:, 0, :, 0:1], gate[0, 0:1, :].rearrange("o (h p) -> p h o", p=P))
-            nc.sync.dma_start(gate_col[:, 1, 0, 0:1], gate[1, 0:1, 0:P].rearrange("o p -> p o"))
+        nc.sync.dma_start(gates[:, :, 0:P], gate[:, 0:P, 0:P].rearrange("d p v -> p d v"))
 
         def picks(lo, hi):
             return offs_t[:, lo // G:hi // G]
@@ -104,6 +101,9 @@ def tile_picked_sub_lin_relu2_sub_e_kernel(tc, xT, w_words, w_scales, b, gate, o
             place_on_vector(3, i * P, (i + 1) * P)
             stage_on_scalar(3, (i + 2) * P, (i + 3) * P)
         pair(nc.scalar.copy, 1, 2 * P, 3 * P)
+        gate_col = sb.tile([P, D, 8], F32, name="gate_col", tag="x3", align_bytes=64)
+        with nc.allow_non_contiguous_dma(reason="one gate value to a partition"):
+            nc.scalar.dma_start(gate_col[:, :, 0:1], gate[:, 0:1, 0:P].rearrange("d o p -> p d o"))
         quantise(0)
         quantise(1)
         pair(nc.vector.tensor_copy, 1, 3 * P, S)
@@ -121,7 +121,6 @@ def tile_picked_sub_lin_relu2_sub_e_kernel(tc, xT, w_words, w_scales, b, gate, o
 
         terms = [sb.tile([P, D, V], F32, name=f"terms{c}", align_bytes=64) for c in range(2)]
         part = sb.tile([P, V], F32, name="part", align_bytes=64)
-        res = [sb.tile([P, V], F32, name=f"res{c}", align_bytes=64) for c in range(2)]
 
         def entries(d, lo, hi):
             return pos_t[d][:, lo // G:hi // G]
@@ -129,35 +128,36 @@ def tile_picked_sub_lin_relu2_sub_e_kernel(tc, xT, w_words, w_scales, b, gate, o
         def fetch_weighted(c, d, lo, hi):
             nc.vector.tensor_tensor(terms[c][:, d, lo:hi], y[c][:].indirect(entries(d, lo, hi)), gates[:, d, lo:hi], ALU.mult)
 
+        later = sb.tile([P, 2, P], F32, name="later", tag="r1", align_bytes=64)
+        plain = (terms[0][:, 0, 0:P], later[:, 0, :], later[:, 1, :])
+
         def fetch_plain(d, lo, hi):
-            nc.scalar.activation(terms[0][:, d, lo:hi], y[0][:].indirect(entries(d, lo, hi)), ACT.Copy)
+            nc.scalar.activation(plain[d], y[0][:].indirect(entries(d, lo, hi)), ACT.Copy)
 
         halves = [slice(h * P, (h + 1) * P) for h in range(2)]
-        steps = ((0, 0), (2, 0), (0, 1), (2, 1), (1, 0))
-        banks = ("bank0_0", "bank0_1", "bank0_2", "bank0_3", "bank1_0")
-        turned = {step: psum.tile([P, P], F32, name=f"turned{step[0]}_{step[1]}", tag=tag) for step, tag in zip(steps, banks)}
-        turned_sb = {step: sb.tile([P, P], F32, name=f"turned_sb{step[0]}_{step[1]}", align_bytes=64) for step in steps}
-        back = [psum.tile([P, P], F32, name=f"back{h}", tag=f"bank1_{1 + h}") for h in range(2)]
+        turned = [psum.tile([P, P], F32, name=f"turned{e}", tag=f"bank0_{e}") for e in range(D + 1)]
+        turned_sb = [sb.tile([P, P], F32, name=f"turned_sb{e}", align_bytes=64) for e in range(D + 1)]
+        res = [sb.tile([P, V], F32, name=f"res{c}", tag=("res0", f"turned_sb{D}")[c], align_bytes=64) for c in range(2)]
+        back = [psum.tile([P, P], F32, name=f"back{h}", tag=f"bank1_{h}") for h in range(2)]
 
-        fetch_plain(0, 0, P)
-        fetch_weighted(0, 2, 0, V)
-        fetch_plain(0, P, V)
-        fetch_weighted(0, 1, P, V)
-        fetch_plain(1, 0, P)
-        for d, h in steps:
-            sources = (2, 1) if (d, h) == (2, 1) else (d,)
-            for e in sources:
-                nc.tensor.matmul(turned[d, h][:], terms[0][:, e, halves[h]], ident[:], start=(e == sources[0]), stop=(e == sources[-1]), is_transpose=True)
-        for d, h in steps:
-            if d == 2:
-                nc.scalar.copy(turned_sb[d, h][:], turned[d, h][:])
+        for d in range(D):
+            fetch_plain(d, 0, P)
+            fetch_weighted(0, d, P, V)
+        nc.tensor.transpose(turned[0][:], plain[0], ident[:])
+        nc.tensor.transpose(turned[1][:], plain[1], ident[:])
+        for d in range(D):
+            nc.tensor.matmul(turned[D][:], terms[0][:, d, halves[1]], ident[:], start=(d == 0), stop=(d == D - 1), is_transpose=True)
+        nc.tensor.transpose(turned[2][:], plain[2], ident[:])
+        for e in (0, 1, D, 2):
+            if e == D:
+                nc.scalar.copy(turned_sb[e][:], turned[e][:])
+                nc.tensor.transpose(back[1][:], turned_sb[e][:], ident[:])
             else:
-                nc.scalar.activation(turned_sb[d, h][:], turned[d, h][:], ACT.Copy, scale=gate_col[:, d, h, 0:1])
-        for d, h in steps:
-            nc.tensor.matmul(back[h][:], turned_sb[d, h][:], ident[:], start=(d == 0), stop=((d, h) in ((2, 1), (1, 0))), is_transpose=True)
+                nc.scalar.activation(turned_sb[e][:], turned[e][:], ACT.Copy, scale=gate_col[:, e, 0:1])
+                nc.tensor.matmul(back[0][:], turned_sb[e][:], ident[:], start=(e == 0), stop=(e == 2), is_transpose=True)
         for h in (1, 0):
             nc.scalar.copy(res[0][:, halves[h]], back[h][:])
-        nc.scalar.dma_start(out[0:P, :], res[0][:])
+            (nc.scalar, nc.sync)[h].dma_start(out[0:P, halves[h]], res[0][:, halves[h]])
 
         fetch_weighted(1, 0, 0, V)
         fetch_weighted(1, 1, 0, V)

@@ -39,7 +39,8 @@ def tile_picked_sub_lin_relu2_sub_e_kernel(tc, xT, w_words, w_scales, b, gate, o
         nc.sync.dma_start(x[0][:], x_rows[:, 0, :])
         nc.sync.dma_start(offs_t[:], offs)
         for q in range(4):
-            nc.scalar.dma_start(plane[32 * q + 4:32 * q + 8, 0:N].bitcast(I32), w_scales[0, 4 * q:4 * q + 4, :].bitcast(I32))
+            twice = w_scales[0, 4 * q:4 * q + 4, :].bitcast(I32).unsqueeze(1).to_broadcast([4, 2, N // 4])
+            nc.scalar.dma_start(plane[32 * q + 4:32 * q + 8, :].bitcast(I32).rearrange("r (e m) -> r e m", e=2), twice)
         ident = sb.tile([P, P], F32, name="ident", align_bytes=64)
         zeros = sb.tile([P, P], F32, name="zeros", align_bytes=64)
         nc.vector.memset(zeros[:], 0.0)
@@ -79,13 +80,17 @@ def tile_picked_sub_lin_relu2_sub_e_kernel(tc, xT, w_words, w_scales, b, gate, o
             source = woven[:, pieces[i], :].rearrange("p n j -> p (n j)")
             nc.vector.quantize_mx(out=codes[:, pieces[i]].bitcast(FP8X4), scales=plane[:, pieces[i]], in_=source)
 
-        acc = [[psum.tile([P, P], F32, name=f"acc{c}_{i}", tag=f"bank{c}_{i}") for i in range(4)] for c in range(2)]
+        def acc_bank(c, i):
+            return f"bank{c}_{i}"
+
+        acc = {}
 
         def product(c, i):
+            acc[c, i] = psum.tile([P, P], F32, name=f"acc{c}_{i}", tag=acc_bank(c, i))
             nc.tensor.matmul_mx(
-                out=acc[c][i][:],
+                out=acc[c, i][:],
                 lhsT=w_codes[:, c * P:(c + 1) * P].bitcast(FP8X4),
-                lhsT_scale=plane[4:P, c * P:(c + 1) * P],
+                lhsT_scale=plane[4:P, pieces[i // 2 * 2 + c]],
                 rhs=codes[:, pieces[i]].bitcast(FP8X4),
                 rhs_scale=plane[:, pieces[i]],
                 start=True,
@@ -109,61 +114,65 @@ def tile_picked_sub_lin_relu2_sub_e_kernel(tc, xT, w_words, w_scales, b, gate, o
         pair(nc.vector.tensor_copy, 1, 3 * P, S)
         quantise(2)
         quantise(3)
-        for c, i in ((0, 0), (1, 0), (0, 1), (1, 1), (0, 2), (0, 3), (1, 2), (1, 3)):
-            product(c, i)
-
         r = [sb.tile([P, S], F32, name=f"r{c}", tag=("staged1", "r1")[c], align_bytes=64) for c in range(2)]
         y = [sb.tile([P, S], F32, name=f"y{c}", tag=("woven", "y1")[c], align_bytes=64) for c in range(2)]
         for c, i in ((0, 0), (1, 0), (0, 1), (1, 1), (0, 2), (0, 3), (1, 2), (1, 3)):
-            nc.scalar.activation(r[c][:, pieces[i]], acc[c][i][:], ACT.Relu, bias=bias[:, c, 0:1])
-        for c, i in ((0, 0), (1, 0), (0, 1), (1, 1), (0, 2), (0, 3), (1, 2), (1, 3)):
+            product(c, i)
+            nc.scalar.activation(r[c][:, pieces[i]], acc[c, i][:], ACT.Relu, bias=bias[:, c, 0:1])
+        for c, i in ((0, 0), (1, 0), (0, 1), (1, 1), (0, 2), (0, 3)):
             nc.vector.tensor_tensor(y[c][:, pieces[i]], r[c][:, pieces[i]], r[c][:, pieces[i]], ALU.mult)
+        for i in (2, 3):
+            nc.scalar.activation(y[1][:, pieces[i]], r[1][:, pieces[i]], ACT.Square)
 
-        terms = [sb.tile([P, D, V], F32, name=f"terms{c}", align_bytes=64) for c in range(2)]
+        terms = sb.tile([P, D, V], F32, name="terms", align_bytes=64)
+        weighted = [sb.tile([P, P], F32, name=f"weighted{d}", align_bytes=64) for d in range(D)]
         part = sb.tile([P, V], F32, name="part", align_bytes=64)
 
         def entries(d, lo, hi):
             return pos_t[d][:, lo // G:hi // G]
 
-        def fetch_weighted(c, d, lo, hi):
-            nc.vector.tensor_tensor(terms[c][:, d, lo:hi], y[c][:].indirect(entries(d, lo, hi)), gates[:, d, lo:hi], ALU.mult)
+        def fetch_weighted(term, c, d, lo, hi):
+            nc.vector.tensor_tensor(term, y[c][:].indirect(entries(d, lo, hi)), gates[:, d, lo:hi], ALU.mult)
 
-        later = sb.tile([P, 2, P], F32, name="later", tag="r1", align_bytes=64)
-        plain = (terms[0][:, 0, 0:P], later[:, 0, :], later[:, 1, :])
+        plain = [sb.tile([P, P], F32, name=f"plain{d}", align_bytes=64) for d in range(D)]
 
         def fetch_plain(d, lo, hi):
-            nc.scalar.activation(plain[d], y[0][:].indirect(entries(d, lo, hi)), ACT.Copy)
+            nc.scalar.activation(plain[d][:], y[0][:].indirect(entries(d, lo, hi)), ACT.Copy)
 
         halves = [slice(h * P, (h + 1) * P) for h in range(2)]
-        turned = [psum.tile([P, P], F32, name=f"turned{e}", tag=f"bank0_{e}") for e in range(D + 1)]
-        turned_sb = [sb.tile([P, P], F32, name=f"turned_sb{e}", align_bytes=64) for e in range(D + 1)]
-        res = [sb.tile([P, V], F32, name=f"res{c}", tag=("res0", f"turned_sb{D}")[c], align_bytes=64) for c in range(2)]
-        back = [psum.tile([P, P], F32, name=f"back{h}", tag=f"bank1_{h}") for h in range(2)]
+        turned = [psum.tile([P, P], F32, name=f"turned{e}", tag=("bank0_0", "bank0_2", "bank0_3", "bank1_0")[e]) for e in range(D + 1)]
+        scaled = sb.tile([P, D, P], F32, name="scaled", tag="woven", align_bytes=64)
+        summed = sb.tile([P, P], F32, name="summed", align_bytes=64)
+        turned_sb = [scaled[:, d, :] for d in range(D)] + [summed[:]]
+        res = [sb.tile([P, V], F32, name=f"res{c}", tag=("res0", "summed")[c], align_bytes=64) for c in range(2)]
+        back = [psum.tile([P, P], F32, name=f"back{h}", tag=("bank1_3", "bank1_1")[h]) for h in range(2)]
 
         for d in range(D):
+            fetch_weighted(weighted[d][:], 0, d, P, V)
+        for d in range(2):
             fetch_plain(d, 0, P)
-            fetch_weighted(0, d, P, V)
-        nc.tensor.transpose(turned[0][:], plain[0], ident[:])
-        nc.tensor.transpose(turned[1][:], plain[1], ident[:])
+        nc.tensor.transpose(turned[0][:], plain[0][:], ident[:])
         for d in range(D):
-            nc.tensor.matmul(turned[D][:], terms[0][:, d, halves[1]], ident[:], start=(d == 0), stop=(d == D - 1), is_transpose=True)
-        nc.tensor.transpose(turned[2][:], plain[2], ident[:])
-        for e in (0, 1, D, 2):
+            nc.tensor.matmul(turned[D][:], weighted[d][:], ident[:], start=(d == 0), stop=(d == D - 1), is_transpose=True)
+        fetch_plain(2, 0, P)
+        nc.tensor.transpose(turned[1][:], plain[1][:], ident[:])
+        nc.tensor.transpose(turned[2][:], plain[2][:], ident[:])
+        for e in (0, D, 1, 2):
             if e == D:
-                nc.scalar.copy(turned_sb[e][:], turned[e][:])
-                nc.tensor.transpose(back[1][:], turned_sb[e][:], ident[:])
+                nc.scalar.copy(turned_sb[e], turned[e][:])
+                nc.tensor.transpose(back[1][:], turned_sb[e], ident[:])
             else:
-                nc.scalar.activation(turned_sb[e][:], turned[e][:], ACT.Copy, scale=gate_col[:, e, 0:1])
-                nc.tensor.matmul(back[0][:], turned_sb[e][:], ident[:], start=(e == 0), stop=(e == 2), is_transpose=True)
+                nc.scalar.activation(turned_sb[e], turned[e][:], ACT.Copy, scale=gate_col[:, e, 0:1])
+                nc.tensor.matmul(back[0][:], turned_sb[e], ident[:], start=(e == 0), stop=(e == 2), is_transpose=True)
         for h in (1, 0):
             nc.scalar.copy(res[0][:, halves[h]], back[h][:])
             (nc.scalar, nc.sync)[h].dma_start(out[0:P, halves[h]], res[0][:, halves[h]])
 
-        fetch_weighted(1, 0, 0, V)
-        fetch_weighted(1, 1, 0, V)
-        fetch_weighted(1, 2, 0, 192)
-        nc.vector.tensor_tensor(part[:], terms[1][:, 0, :], terms[1][:, 1, :], ALU.add)
-        fetch_weighted(1, 2, 192, V)
+        fetch_weighted(terms[:, 0, 0:V], 1, 0, 0, V)
+        fetch_weighted(terms[:, 1, 0:V], 1, 1, 0, V)
+        fetch_weighted(terms[:, 2, 0:192], 1, 2, 0, 192)
+        nc.vector.tensor_tensor(part[:], terms[:, 0, :], terms[:, 1, :], ALU.add)
+        fetch_weighted(terms[:, 2, 192:V], 1, 2, 192, V)
         for lo, hi in ((0, 192), (192, V)):
-            nc.vector.tensor_tensor(res[1][:, lo:hi], part[:, lo:hi], terms[1][:, 2, lo:hi], ALU.add)
+            nc.vector.tensor_tensor(res[1][:, lo:hi], part[:, lo:hi], terms[:, 2, lo:hi], ALU.add)
             nc.sync.dma_start(out[P:N, lo:hi], res[1][:, lo:hi])

@@ -33,7 +33,6 @@ def tile_picked_sub_lin_relu2_sub_e_kernel(tc, xT, w_words, w_scales, b, gate, o
         x = [sb.tile([P, T], F32, name=f"x{j}", align_bytes=64) for j in range(4)]
         w_codes = sb.tile([P, N], I32, name="w_codes", align_bytes=64)
         plane = sb.tile([P, S], U8, name="plane", align_bytes=64)
-        bias = sb.tile([P, 2, 8], F32, name="bias")
         gates = sb.tile([P, D, V], F32, name="gates", align_bytes=64)
 
         nc.sync.dma_start(x[0][:], x_rows[:, 0, :])
@@ -43,14 +42,18 @@ def tile_picked_sub_lin_relu2_sub_e_kernel(tc, xT, w_words, w_scales, b, gate, o
             nc.scalar.dma_start(plane[32 * q + 4:32 * q + 8, :].bitcast(I32).rearrange("r (e m) -> r e m", e=2), twice)
         ident = sb.tile([P, P], F32, name="ident", align_bytes=64)
         zeros = sb.tile([P, P], F32, name="zeros", align_bytes=64)
+        rows = sb.tile([P, P], F32, name="rows", align_bytes=64)
         nc.vector.memset(zeros[:], 0.0)
+        nc.vector.memset(rows[0:P - 5, :], 0.0)
         nc.scalar.copy(ident[:], zeros[:])
         make_identity(nc, ident[:], nomemset=True)
         for j in (1, 2, 3):
             nc.sync.dma_start(x[j][:], x_rows[:, j, :])
+        nc.sync.dma_start(rows[P - 2:P, :], b.rearrange("(c p) o -> c (p o)", p=P))
+        nc.sync.dma_start(rows[P - 5:P - 2, :], gate[:, 0, 0:P])
         nc.sync.dma_start(w_codes[:], w_words[0].rearrange("p n t -> p (n t)").bitcast(I32))
-        with nc.allow_non_contiguous_dma(reason="one bias value to a partition"):
-            nc.sync.dma_start(bias[:, :, 0:1], b.rearrange("(c p) o -> p c o", p=P))
+        rows_turned = psum.tile([P, P], F32, name="rows_turned", tag="bank1_3")
+        nc.tensor.transpose(rows_turned[:], rows[:], ident[:])
         nc.sync.dma_start(gates[:, :, P:V], gate[:, 0:P, P:V].rearrange("d p v -> p d v"))
         nc.sync.dma_start(pos_t[0][:], pos1)
         nc.sync.dma_start(pos_t[1][:], pos2)
@@ -106,9 +109,8 @@ def tile_picked_sub_lin_relu2_sub_e_kernel(tc, xT, w_words, w_scales, b, gate, o
             place_on_vector(3, i * P, (i + 1) * P)
             stage_on_scalar(3, (i + 2) * P, (i + 3) * P)
         pair(nc.scalar.copy, 1, 2 * P, 3 * P)
-        gate_col = sb.tile([P, D, 8], F32, name="gate_col", tag="x3", align_bytes=64)
-        with nc.allow_non_contiguous_dma(reason="one gate value to a partition"):
-            nc.scalar.dma_start(gate_col[:, :, 0:1], gate[:, 0:1, 0:P].rearrange("d o p -> p d o"))
+        columns = sb.tile([P, 8], F32, name="columns", tag="x3", align_bytes=64)
+        nc.scalar.copy(columns[:, 0:5], rows_turned[:, P - 5:P])
         quantise(0)
         quantise(1)
         pair(nc.vector.tensor_copy, 1, 3 * P, S)
@@ -118,7 +120,7 @@ def tile_picked_sub_lin_relu2_sub_e_kernel(tc, xT, w_words, w_scales, b, gate, o
         y = [sb.tile([P, S], F32, name=f"y{c}", tag=("woven", "y1")[c], align_bytes=64) for c in range(2)]
         for c, i in ((0, 0), (1, 0), (0, 1), (1, 1), (0, 2), (0, 3), (1, 2), (1, 3)):
             product(c, i)
-            nc.scalar.activation(r[c][:, pieces[i]], acc[c, i][:], ACT.Relu, bias=bias[:, c, 0:1])
+            nc.scalar.activation(r[c][:, pieces[i]], acc[c, i][:], ACT.Relu, bias=columns[:, D + c:D + c + 1])
         for c, i in ((0, 0), (1, 0), (0, 1), (1, 1), (0, 2), (0, 3)):
             nc.vector.tensor_tensor(y[c][:, pieces[i]], r[c][:, pieces[i]], r[c][:, pieces[i]], ALU.mult)
         for i in (2, 3):
@@ -162,7 +164,7 @@ def tile_picked_sub_lin_relu2_sub_e_kernel(tc, xT, w_words, w_scales, b, gate, o
                 nc.scalar.copy(turned_sb[e], turned[e][:])
                 nc.tensor.transpose(back[1][:], turned_sb[e], ident[:])
             else:
-                nc.scalar.activation(turned_sb[e], turned[e][:], ACT.Copy, scale=gate_col[:, e, 0:1])
+                nc.scalar.activation(turned_sb[e], turned[e][:], ACT.Copy, scale=columns[:, e:e + 1])
                 nc.tensor.matmul(back[0][:], turned_sb[e], ident[:], start=(e == 0), stop=(e == 2), is_transpose=True)
         for h in (1, 0):
             nc.scalar.copy(res[0][:, halves[h]], back[h][:])

@@ -25,6 +25,7 @@ def tile_picked_sub_lin_relu2_sub_e_kernel(tc, xT, w_words, w_scales, b, gate, o
     with ExitStack() as ctx:
         lists = ctx.enter_context(tc.tile_pool(name="lists", bufs=1))
         sb = ctx.enter_context(tc.tile_pool(name="sb", bufs=1))
+        reused = ctx.enter_context(tc.tile_pool(name="reused", bufs=1))
         psum = ctx.enter_context(tc.psum_pool(name="psum", bufs=1))
 
         offs_t = lists.tile([P, S // G], U16, name="offs_t")
@@ -32,39 +33,40 @@ def tile_picked_sub_lin_relu2_sub_e_kernel(tc, xT, w_words, w_scales, b, gate, o
         x_rows = xT.rearrange("(p j) t -> p j t", j=4)
         x = [sb.tile([P, T], F32, name=f"x{j}", align_bytes=64) for j in range(4)]
         w_codes = sb.tile([P, N], I32, name="w_codes", align_bytes=64)
-        plane = sb.tile([P, S], U8, name="plane", align_bytes=64)
+        w_plane = sb.tile([P, N], U8, name="w_plane", align_bytes=64)
+        x_plane = sb.tile([P, S], U8, name="x_plane", align_bytes=64)
         gates = sb.tile([P, D, V], F32, name="gates", align_bytes=64)
+        bias = sb.tile([P, 2], F32, name="bias", align_bytes=64)
+        gate_cols = sb.tile([P, D], F32, name="gate_cols", align_bytes=64)
 
         nc.sync.dma_start(x[0][:], x_rows[:, 0, :])
         nc.sync.dma_start(offs_t[:], offs)
-        for q in range(4):
-            twice = w_scales[0, 4 * q:4 * q + 4, :].bitcast(I32).unsqueeze(1).to_broadcast([4, 2, N // 4])
-            nc.scalar.dma_start(plane[32 * q + 4:32 * q + 8, :].bitcast(I32).rearrange("r (e m) -> r e m", e=2), twice)
-        ident = sb.tile([P, P], F32, name="ident", align_bytes=64)
-        zeros = sb.tile([P, P], F32, name="zeros", align_bytes=64)
-        rows = sb.tile([P, P], F32, name="rows", align_bytes=64)
-        nc.vector.memset(zeros[:], 0.0)
-        nc.vector.memset(rows[0:P - 5, :], 0.0)
-        nc.scalar.copy(ident[:], zeros[:])
-        make_identity(nc, ident[:], nomemset=True)
         for j in (1, 2, 3):
             nc.sync.dma_start(x[j][:], x_rows[:, j, :])
-        nc.sync.dma_start(rows[P - 2:P, :], b.rearrange("(c p) o -> c (p o)", p=P))
-        nc.sync.dma_start(rows[P - 5:P - 2, :], gate[:, 0, 0:P])
         nc.sync.dma_start(w_codes[:], w_words[0].rearrange("p n t -> p (n t)").bitcast(I32))
-        rows_turned = psum.tile([P, P], F32, name="rows_turned", tag="bank1_3")
-        nc.tensor.transpose(rows_turned[:], rows[:], ident[:])
+        for q in range(4):
+            rows = w_scales[0, 4 * q:4 * q + 4, :].bitcast(I32).unsqueeze(0).to_broadcast([8, 4, N // 4])
+            nc.sync.dma_start(w_plane[32 * q:32 * q + 32, :].bitcast(I32), rows)
+        with nc.allow_non_contiguous_dma(reason="one bias value a partition"):
+            nc.sync.dma_start(bias[:], b.rearrange("(c p) o -> p (c o)", p=P))
+        with nc.allow_non_contiguous_dma(reason="one gate value a partition"):
+            nc.sync.dma_start(gate_cols[:], gate[:, 0, 0:P].rearrange("d v -> v d"))
         nc.sync.dma_start(gates[:, :, P:V], gate[:, 0:P, P:V].rearrange("d p v -> p d v"))
-        nc.sync.dma_start(pos_t[0][:], pos1)
-        nc.sync.dma_start(pos_t[1][:], pos2)
-        nc.sync.dma_start(pos_t[2][:], pos3)
+        for d, pos in enumerate((pos1, pos2, pos3)):
+            nc.sync.dma_start(pos_t[d][:], pos)
         nc.sync.dma_start(gates[:, :, 0:P], gate[:, 0:P, 0:P].rearrange("d p v -> p d v"))
+
+        ident = sb.tile([P, P], F32, name="ident", align_bytes=64)
+        zeros = sb.tile([P, P], F32, name="zeros", align_bytes=64)
+        nc.vector.memset(zeros[:], 0.0)
+        nc.scalar.copy(ident[:], zeros[:])
+        make_identity(nc, ident[:], nomemset=True)
 
         def picks(lo, hi):
             return offs_t[:, lo // G:hi // G]
 
         W = (384, 256)
-        woven = sb.tile([P, S, 4], BF16, name="woven", align_bytes=64)
+        woven = reused.tile([P, S, 4], BF16, name="woven", align_bytes=64, offset=0)
         staged = [sb.tile([P, 2, S - W[u]], BF16, name=f"staged{u}", align_bytes=64) for u in range(2)]
         codes = sb.tile([P, S], U32, name="codes", align_bytes=64)
         pieces = [slice(i * P, (i + 1) * P) for i in range(4)]
@@ -81,21 +83,18 @@ def tile_picked_sub_lin_relu2_sub_e_kernel(tc, xT, w_words, w_scales, b, gate, o
 
         def quantise(i):
             source = woven[:, pieces[i], :].rearrange("p n j -> p (n j)")
-            nc.vector.quantize_mx(out=codes[:, pieces[i]].bitcast(FP8X4), scales=plane[:, pieces[i]], in_=source)
-
-        def acc_bank(c, i):
-            return f"bank{c}_{i}"
+            nc.vector.quantize_mx(out=codes[:, pieces[i]].bitcast(FP8X4), scales=x_plane[:, pieces[i]], in_=source)
 
         acc = {}
 
         def product(c, i):
-            acc[c, i] = psum.tile([P, P], F32, name=f"acc{c}_{i}", tag=acc_bank(c, i))
+            acc[c, i] = psum.tile([P, P], F32, name=f"acc{c}_{i}", tag=f"bank{c}_{i}")
             nc.tensor.matmul_mx(
                 out=acc[c, i][:],
                 lhsT=w_codes[:, c * P:(c + 1) * P].bitcast(FP8X4),
-                lhsT_scale=plane[4:P, pieces[i // 2 * 2 + c]],
+                lhsT_scale=w_plane[:, c * P:(c + 1) * P],
                 rhs=codes[:, pieces[i]].bitcast(FP8X4),
-                rhs_scale=plane[:, pieces[i]],
+                rhs_scale=x_plane[:, pieces[i]],
                 start=True,
                 stop=True,
             )
@@ -109,26 +108,45 @@ def tile_picked_sub_lin_relu2_sub_e_kernel(tc, xT, w_words, w_scales, b, gate, o
             place_on_vector(3, i * P, (i + 1) * P)
             stage_on_scalar(3, (i + 2) * P, (i + 3) * P)
         pair(nc.scalar.copy, 1, 2 * P, 3 * P)
-        columns = sb.tile([P, 8], F32, name="columns", tag="x3", align_bytes=64)
-        nc.scalar.copy(columns[:, 0:5], rows_turned[:, P - 5:P])
         quantise(0)
         quantise(1)
         pair(nc.vector.tensor_copy, 1, 3 * P, S)
         quantise(2)
         quantise(3)
-        r = [sb.tile([P, S], F32, name=f"r{c}", tag=("staged1", "r1")[c], align_bytes=64) for c in range(2)]
-        y = [sb.tile([P, S], F32, name=f"y{c}", tag=("woven", "y1")[c], align_bytes=64) for c in range(2)]
-        for c, i in ((0, 0), (1, 0), (0, 1), (1, 1), (0, 2), (0, 3), (1, 2), (1, 3)):
-            product(c, i)
-            nc.scalar.activation(r[c][:, pieces[i]], acc[c, i][:], ACT.Relu, bias=columns[:, D + c:D + c + 1])
-        for c, i in ((0, 0), (1, 0), (0, 1), (1, 1), (0, 2), (0, 3)):
+
+        r = [sb.tile([P, S], F32, name="r0", tag="staged1", align_bytes=64), reused.tile([P, S], F32, name="r1", align_bytes=64, offset=4 * S)]
+        y = [reused.tile([P, S], F32, name="y0", align_bytes=64, offset=0), sb.tile([P, S], F32, name="y1", tag="codes", align_bytes=64)]
+
+        def relu_on_scalar(c, i):
+            nc.scalar.activation(r[c][:, pieces[i]], acc[c, i][:], ACT.Relu, bias=bias[:, c:c + 1])
+
+        def relu_on_vector(c, i):
+            nc.vector.tensor_scalar(r[c][:, pieces[i]], acc[c, i][:], bias[:, c:c + 1], 0.0, ALU.add, ALU.max)
+
+        def square_on_vector(c, i):
             nc.vector.tensor_tensor(y[c][:, pieces[i]], r[c][:, pieces[i]], r[c][:, pieces[i]], ALU.mult)
-        for i in (2, 3):
-            nc.scalar.activation(y[1][:, pieces[i]], r[1][:, pieces[i]], ACT.Square)
+
+        def square_on_scalar(c, i):
+            nc.scalar.activation(y[c][:, pieces[i]], r[c][:, pieces[i]], ACT.Square)
+
+        for i in range(4):
+            for c in range(2):
+                product(c, i)
+        for c, i in ((0, 0), (0, 1), (1, 0), (0, 2), (0, 3), (1, 3)):
+            relu_on_scalar(c, i)
+        square_on_vector(0, 0)
+        relu_on_vector(1, 1)
+        square_on_vector(0, 1)
+        relu_on_vector(1, 2)
+        for c, i in ((0, 2), (0, 3), (1, 3)):
+            square_on_vector(c, i)
+        for i in range(3):
+            square_on_scalar(1, i)
 
         terms = sb.tile([P, D, V], F32, name="terms", align_bytes=64)
         weighted = [sb.tile([P, P], F32, name=f"weighted{d}", align_bytes=64) for d in range(D)]
         part = sb.tile([P, V], F32, name="part", align_bytes=64)
+        plain = [sb.tile([P, P], F32, name=f"plain{d}", align_bytes=64) for d in range(D)]
 
         def entries(d, lo, hi):
             return pos_t[d][:, lo // G:hi // G]
@@ -136,14 +154,12 @@ def tile_picked_sub_lin_relu2_sub_e_kernel(tc, xT, w_words, w_scales, b, gate, o
         def fetch_weighted(term, c, d, lo, hi):
             nc.vector.tensor_tensor(term, y[c][:].indirect(entries(d, lo, hi)), gates[:, d, lo:hi], ALU.mult)
 
-        plain = [sb.tile([P, P], F32, name=f"plain{d}", align_bytes=64) for d in range(D)]
-
         def fetch_plain(d, lo, hi):
             nc.scalar.activation(plain[d][:], y[0][:].indirect(entries(d, lo, hi)), ACT.Copy)
 
         halves = [slice(h * P, (h + 1) * P) for h in range(2)]
         turned = [psum.tile([P, P], F32, name=f"turned{e}", tag=("bank0_0", "bank0_2", "bank0_3", "bank1_0")[e]) for e in range(D + 1)]
-        scaled = sb.tile([P, D, P], F32, name="scaled", tag="woven", align_bytes=64)
+        scaled = reused.tile([P, D, P], F32, name="scaled", align_bytes=64, offset=0)
         summed = sb.tile([P, P], F32, name="summed", align_bytes=64)
         turned_sb = [scaled[:, d, :] for d in range(D)] + [summed[:]]
         res = [sb.tile([P, V], F32, name=f"res{c}", tag=("res0", "summed")[c], align_bytes=64) for c in range(2)]
@@ -164,7 +180,7 @@ def tile_picked_sub_lin_relu2_sub_e_kernel(tc, xT, w_words, w_scales, b, gate, o
                 nc.scalar.copy(turned_sb[e], turned[e][:])
                 nc.tensor.transpose(back[1][:], turned_sb[e], ident[:])
             else:
-                nc.scalar.activation(turned_sb[e], turned[e][:], ACT.Copy, scale=columns[:, e:e + 1])
+                nc.scalar.activation(turned_sb[e], turned[e][:], ACT.Copy, scale=gate_cols[:, e:e + 1])
                 nc.tensor.matmul(back[0][:], turned_sb[e], ident[:], start=(e == 0), stop=(e == 2), is_transpose=True)
         for h in (1, 0):
             nc.scalar.copy(res[0][:, halves[h]], back[h][:])

@@ -36,21 +36,20 @@ def tile_picked_sub_lin_relu2_sub_e_kernel(tc, xT, w_words, w_scales, b, gate, o
         w_plane = sb.tile([P, N], U8, name="w_plane", align_bytes=64)
         x_plane = sb.tile([P, S], U8, name="x_plane", align_bytes=64)
         gates = sb.tile([P, D, V], F32, name="gates", align_bytes=64)
-        bias = sb.tile([P, 2], F32, name="bias", align_bytes=64)
-        gate_cols = sb.tile([P, D], F32, name="gate_cols", align_bytes=64)
+        rows = sb.tile([P, P], F32, name="rows", align_bytes=64)
+        columns = sb.tile([P, 8], F32, name="columns", align_bytes=64)
 
         nc.sync.dma_start(x[0][:], x_rows[:, 0, :])
         nc.sync.dma_start(offs_t[:], offs)
+        nc.scalar.dma_start(rows[P - 2:P, :], b.rearrange("(c p) o -> c (p o)", p=P))
+        nc.scalar.dma_start(rows[P - 5:P - 3, :], gate[0:2, 0, 0:P])
+        nc.scalar.dma_start(rows[P - 3:P - 2, :], gate[2, 0:1, 0:P])
         for j in (1, 2, 3):
             nc.sync.dma_start(x[j][:], x_rows[:, j, :])
         nc.sync.dma_start(w_codes[:], w_words[0].rearrange("p n t -> p (n t)").bitcast(I32))
         for q in range(4):
-            rows = w_scales[0, 4 * q:4 * q + 4, :].bitcast(I32).unsqueeze(0).to_broadcast([8, 4, N // 4])
-            nc.sync.dma_start(w_plane[32 * q:32 * q + 32, :].bitcast(I32), rows)
-        with nc.allow_non_contiguous_dma(reason="one bias value a partition"):
-            nc.sync.dma_start(bias[:], b.rearrange("(c p) o -> p (c o)", p=P))
-        with nc.allow_non_contiguous_dma(reason="one gate value a partition"):
-            nc.sync.dma_start(gate_cols[:], gate[:, 0, 0:P].rearrange("d v -> v d"))
+            repeated = w_scales[0, 4 * q:4 * q + 4, :].bitcast(I32).unsqueeze(0).to_broadcast([8, 4, N // 4])
+            nc.sync.dma_start(w_plane[32 * q:32 * q + 32, :].bitcast(I32), repeated)
         nc.sync.dma_start(gates[:, :, P:V], gate[:, 0:P, P:V].rearrange("d p v -> p d v"))
         for d, pos in enumerate((pos1, pos2, pos3)):
             nc.sync.dma_start(pos_t[d][:], pos)
@@ -61,6 +60,10 @@ def tile_picked_sub_lin_relu2_sub_e_kernel(tc, xT, w_words, w_scales, b, gate, o
         nc.vector.memset(zeros[:], 0.0)
         nc.scalar.copy(ident[:], zeros[:])
         make_identity(nc, ident[:], nomemset=True)
+        nc.vector.memset(rows[0:P - 5, :], 0.0)
+        rows_turned = psum.tile([P, P], F32, name="rows_turned", tag="bank1_3")
+        nc.tensor.transpose(rows_turned[:], rows[:], ident[:])
+        nc.scalar.copy(columns[:, 0:5], rows_turned[:, P - 5:P])
 
         def picks(lo, hi):
             return offs_t[:, lo // G:hi // G]
@@ -118,10 +121,10 @@ def tile_picked_sub_lin_relu2_sub_e_kernel(tc, xT, w_words, w_scales, b, gate, o
         y = [reused.tile([P, S], F32, name="y0", align_bytes=64, offset=0), sb.tile([P, S], F32, name="y1", tag="codes", align_bytes=64)]
 
         def relu_on_scalar(c, i):
-            nc.scalar.activation(r[c][:, pieces[i]], acc[c, i][:], ACT.Relu, bias=bias[:, c:c + 1])
+            nc.scalar.activation(r[c][:, pieces[i]], acc[c, i][:], ACT.Relu, bias=columns[:, D + c:D + c + 1])
 
         def relu_on_vector(c, i):
-            nc.vector.tensor_scalar(r[c][:, pieces[i]], acc[c, i][:], bias[:, c:c + 1], 0.0, ALU.add, ALU.max)
+            nc.vector.tensor_scalar(r[c][:, pieces[i]], acc[c, i][:], columns[:, D + c:D + c + 1], 0.0, ALU.add, ALU.max)
 
         def square_on_vector(c, i):
             nc.vector.tensor_tensor(y[c][:, pieces[i]], r[c][:, pieces[i]], r[c][:, pieces[i]], ALU.mult)
@@ -180,7 +183,7 @@ def tile_picked_sub_lin_relu2_sub_e_kernel(tc, xT, w_words, w_scales, b, gate, o
                 nc.scalar.copy(turned_sb[e], turned[e][:])
                 nc.tensor.transpose(back[1][:], turned_sb[e], ident[:])
             else:
-                nc.scalar.activation(turned_sb[e], turned[e][:], ACT.Copy, scale=gate_cols[:, e:e + 1])
+                nc.scalar.activation(turned_sb[e], turned[e][:], ACT.Copy, scale=columns[:, e:e + 1])
                 nc.tensor.matmul(back[0][:], turned_sb[e], ident[:], start=(e == 0), stop=(e == 2), is_transpose=True)
         for h in (1, 0):
             nc.scalar.copy(res[0][:, halves[h]], back[h][:])

@@ -37,15 +37,13 @@ def tile_picked_sub_lin_relu2_sub_e_kernel(tc, xT, w_words, w_scales, b, gate, o
         x_plane = sb.tile([P, S], U8, name="x_plane", align_bytes=64)
         gates = sb.tile([P, D, V], F32, name="gates", align_bytes=64)
         rows = sb.tile([P, P], F32, name="rows", align_bytes=64)
-        columns = sb.tile([P, 8], F32, name="columns", align_bytes=64)
 
         nc.sync.dma_start(x[0][:], x_rows[:, 0, :])
         nc.sync.dma_start(offs_t[:], offs)
-        nc.scalar.dma_start(rows[P - 2:P, :], b.rearrange("(c p) o -> c (p o)", p=P))
-        nc.scalar.dma_start(rows[P - 5:P - 3, :], gate[0:2, 0, 0:P])
-        nc.scalar.dma_start(rows[P - 3:P - 2, :], gate[2, 0:1, 0:P])
         for j in (1, 2, 3):
             nc.sync.dma_start(x[j][:], x_rows[:, j, :])
+        nc.sync.dma_start(rows[P - 2:P, :], b.rearrange("(c p) o -> c (p o)", p=P))
+        nc.sync.dma_start(rows[P - 5:P - 2, :], gate[:, 0, 0:P])
         nc.sync.dma_start(w_codes[:], w_words[0].rearrange("p n t -> p (n t)").bitcast(I32))
         for q in range(4):
             repeated = w_scales[0, 4 * q:4 * q + 4, :].bitcast(I32).unsqueeze(0).to_broadcast([8, 4, N // 4])
@@ -63,7 +61,6 @@ def tile_picked_sub_lin_relu2_sub_e_kernel(tc, xT, w_words, w_scales, b, gate, o
         nc.vector.memset(rows[0:P - 5, :], 0.0)
         rows_turned = psum.tile([P, P], F32, name="rows_turned", tag="bank1_3")
         nc.tensor.transpose(rows_turned[:], rows[:], ident[:])
-        nc.scalar.copy(columns[:, 0:5], rows_turned[:, P - 5:P])
 
         def picks(lo, hi):
             return offs_t[:, lo // G:hi // G]
@@ -111,6 +108,8 @@ def tile_picked_sub_lin_relu2_sub_e_kernel(tc, xT, w_words, w_scales, b, gate, o
             place_on_vector(3, i * P, (i + 1) * P)
             stage_on_scalar(3, (i + 2) * P, (i + 3) * P)
         pair(nc.scalar.copy, 1, 2 * P, 3 * P)
+        columns = sb.tile([P, 8], F32, name="columns", tag="x3", align_bytes=64)
+        nc.scalar.copy(columns[:, 0:5], rows_turned[:, P - 5:P])
         quantise(0)
         quantise(1)
         pair(nc.vector.tensor_copy, 1, 3 * P, S)

@@ -65,7 +65,7 @@ def tile_picked_sub_lin_relu2_sub_e_kernel(tc, xT, w_words, w_scales, b, gate, o
         def picks(lo, hi):
             return offs_t[:, lo // G:hi // G]
 
-        W = (384, 256)
+        W = (320, 256)
         woven = reused.tile([P, S, 4], BF16, name="woven", align_bytes=64, offset=0)
         staged = [sb.tile([P, 2, S - W[u]], BF16, name=f"staged{u}", align_bytes=64) for u in range(2)]
         codes = sb.tile([P, S], U32, name="codes", align_bytes=64)

from contextlib import ExitStack

import concourse.mybir as mybir
from concourse.masks import make_identity

K, T, D, S, V, N = 512, 1024, 3, 512, 256, 256
FLOPS = 2 * K * S * N

F32 = mybir.dt.float32
BF16 = mybir.dt.bfloat16
I32 = mybir.dt.int32
U16 = mybir.dt.uint16
U32 = mybir.dt.uint32
U8 = mybir.dt.uint8
FP8X4 = mybir.dt.float8_e4m3fn_x4
ACT = mybir.ActivationFunctionType
ALU = mybir.AluOpType

P = 128
G = 16


def tile_picked_sub_lin_relu2_sub_e_kernel(tc, xT, w_words, w_scales, b, gate, offs, pos1, pos2, pos3, out):
    nc = tc.nc
    with ExitStack() as ctx:
        lists = ctx.enter_context(tc.tile_pool(name="lists", bufs=1))
        sb = ctx.enter_context(tc.tile_pool(name="sb", bufs=1))
        reused = ctx.enter_context(tc.tile_pool(name="reused", bufs=1))
        psum = ctx.enter_context(tc.psum_pool(name="psum", bufs=1))

        offs_t = lists.tile([P, S // G], U16, name="offs_t")
        pos_t = [lists.tile([P, V // G], U16, name=f"pos_t{d}") for d in range(D)]
        x_rows = xT.rearrange("(p j) t -> p j t", j=4)
        x = [sb.tile([P, T], F32, name=f"x{j}", align_bytes=64) for j in range(4)]
        w_codes = sb.tile([P, N], I32, name="w_codes", align_bytes=64)
        w_plane = sb.tile([P, N], U8, name="w_plane", align_bytes=64)
        x_plane = sb.tile([P, S], U8, name="x_plane", align_bytes=64)
        gates = sb.tile([P, D, V], F32, name="gates", align_bytes=64)
        rows = sb.tile([P, P], F32, name="rows", align_bytes=64)

        nc.sync.dma_start(x[0][:], x_rows[:, 0, :])
        nc.sync.dma_start(offs_t[:], offs)
        for j in (1, 2, 3):
            nc.sync.dma_start(x[j][:], x_rows[:, j, :])
        nc.sync.dma_start(rows[P - 2:P, :], b.rearrange("(c p) o -> c (p o)", p=P))
        nc.sync.dma_start(rows[P - 5:P - 2, :], gate[:, 0, 0:P])
        nc.sync.dma_start(w_codes[:], w_words[0].rearrange("p n t -> p (n t)").bitcast(I32))
        for q in range(4):
            repeated = w_scales[0, 4 * q:4 * q + 4, :].bitcast(I32).unsqueeze(0).to_broadcast([8, 4, N // 4])
            nc.sync.dma_start(w_plane[32 * q:32 * q + 32, :].bitcast(I32), repeated)
        nc.sync.dma_start(gates[:, :, P:V], gate[:, 0:P, P:V].rearrange("d p v -> p d v"))
        for d, pos in enumerate((pos1, pos2, pos3)):
            nc.sync.dma_start(pos_t[d][:], pos)
        nc.sync.dma_start(gates[:, :, 0:P], gate[:, 0:P, 0:P].rearrange("d p v -> p d v"))

        ident = sb.tile([P, P], F32, name="ident", align_bytes=64)
        zeros = sb.tile([P, P], F32, name="zeros", align_bytes=64)
        nc.vector.memset(zeros[:], 0.0)
        nc.scalar.copy(ident[:], zeros[:])
        make_identity(nc, ident[:], nomemset=True)
        nc.vector.memset(rows[0:P - 5, :], 0.0)
        rows_turned = psum.tile([P, P], F32, name="rows_turned", tag="bank1_3")
        nc.tensor.transpose(rows_turned[:], rows[:], ident[:])

        def picks(lo, hi):
            return offs_t[:, lo // G:hi // G]

        W = (320, 256)
        woven = reused.tile([P, S, 4], BF16, name="woven", align_bytes=64, offset=0)
        staged = [sb.tile([P, 2, S - W[u]], BF16, name=f"staged{u}", align_bytes=64) for u in range(2)]
        codes = sb.tile([P, S], U32, name="codes", align_bytes=64)
        pieces = [slice(i * P, (i + 1) * P) for i in range(4)]

        def stage_on_scalar(j, lo, hi):
            first = W[j // 2]
            nc.scalar.activation(staged[j // 2][:, j % 2, lo - first:hi - first], x[j][:].indirect(picks(lo, hi)), ACT.Copy)

        def pair(copy, u, lo, hi):
            copy(woven[:, lo:hi, 2 * u:2 * u + 2], staged[u][:, :, lo - W[u]:hi - W[u]].rearrange("p j n -> p n j"))

        def place_on_vector(j, lo, hi):
            nc.vector.tensor_copy(woven[:, lo:hi, j], x[j][:].indirect(picks(lo, hi)))

        def quantise(i):
            source = woven[:, pieces[i], :].rearrange("p n j -> p (n j)")
            nc.vector.quantize_mx(out=codes[:, pieces[i]].bitcast(FP8X4), scales=x_plane[:, pieces[i]], in_=source)

        acc = {}

        def product(c, i):
            acc[c, i] = psum.tile([P, P], F32, name=f"acc{c}_{i}", tag=f"bank{c}_{i}")
            nc.tensor.matmul_mx(
                out=acc[c, i][:],
                lhsT=w_codes[:, c * P:(c + 1) * P].bitcast(FP8X4),
                lhsT_scale=w_plane[:, c * P:(c + 1) * P],
                rhs=codes[:, pieces[i]].bitcast(FP8X4),
                rhs_scale=x_plane[:, pieces[i]],
                start=True,
                stop=True,
            )

        for j in range(3):
            place_on_vector(j, 0, W[j // 2])
            stage_on_scalar(j, W[j // 2], S)
            if j == 1:
                pair(nc.scalar.copy, 0, W[0], S)
        for i in (0, 1):
            place_on_vector(3, i * P, (i + 1) * P)
            stage_on_scalar(3, (i + 2) * P, (i + 3) * P)
        pair(nc.scalar.copy, 1, 2 * P, 3 * P)
        columns = sb.tile([P, 8], F32, name="columns", tag="x3", align_bytes=64)
        nc.scalar.copy(columns[:, 0:5], rows_turned[:, P - 5:P])
        quantise(0)
        quantise(1)
        pair(nc.vector.tensor_copy, 1, 3 * P, S)
        quantise(2)
        quantise(3)

        r = [sb.tile([P, S], F32, name="r0", tag="staged1", align_bytes=64), reused.tile([P, S], F32, name="r1", align_bytes=64, offset=4 * S)]
        y = [reused.tile([P, S], F32, name="y0", align_bytes=64, offset=0), sb.tile([P, S], F32, name="y1", tag="codes", align_bytes=64)]

        def relu_on_scalar(c, i):
            nc.scalar.activation(r[c][:, pieces[i]], acc[c, i][:], ACT.Relu, bias=columns[:, D + c:D + c + 1])

        def relu_on_vector(c, i):
            nc.vector.tensor_scalar(r[c][:, pieces[i]], acc[c, i][:], columns[:, D + c:D + c + 1], 0.0, ALU.add, ALU.max)

        def square_on_vector(c, i):
            nc.vector.tensor_tensor(y[c][:, pieces[i]], r[c][:, pieces[i]], r[c][:, pieces[i]], ALU.mult)

        def square_on_scalar(c, i):
            nc.scalar.activation(y[c][:, pieces[i]], r[c][:, pieces[i]], ACT.Square)

        for i in range(4):
            for c in range(2):
                product(c, i)
        for c, i in ((0, 0), (0, 1), (1, 0), (0, 2), (0, 3), (1, 3)):
            relu_on_scalar(c, i)
        square_on_vector(0, 0)
        relu_on_vector(1, 1)
        square_on_vector(0, 1)
        relu_on_vector(1, 2)
        for c, i in ((0, 2), (0, 3), (1, 3)):
            square_on_vector(c, i)
        for i in range(3):
            square_on_scalar(1, i)

        terms = sb.tile([P, D, V], F32, name="terms", align_bytes=64)
        weighted = [sb.tile([P, P], F32, name=f"weighted{d}", align_bytes=64) for d in range(D)]
        part = sb.tile([P, V], F32, name="part", align_bytes=64)
        plain = [sb.tile([P, P], F32, name=f"plain{d}", align_bytes=64) for d in range(D)]

        def entries(d, lo, hi):
            return pos_t[d][:, lo // G:hi // G]

        def fetch_weighted(term, c, d, lo, hi):
            nc.vector.tensor_tensor(term, y[c][:].indirect(entries(d, lo, hi)), gates[:, d, lo:hi], ALU.mult)

        def fetch_plain(d, lo, hi):
            nc.scalar.activation(plain[d][:], y[0][:].indirect(entries(d, lo, hi)), ACT.Copy)

        halves = [slice(h * P, (h + 1) * P) for h in range(2)]
        turned = [psum.tile([P, P], F32, name=f"turned{e}", tag=("bank0_0", "bank0_2", "bank0_3", "bank1_0")[e]) for e in range(D + 1)]
        scaled = reused.tile([P, D, P], F32, name="scaled", align_bytes=64, offset=0)
        summed = sb.tile([P, P], F32, name="summed", align_bytes=64)
        turned_sb = [scaled[:, d, :] for d in range(D)] + [summed[:]]
        res = [sb.tile([P, V], F32, name=f"res{c}", tag=("res0", "summed")[c], align_bytes=64) for c in range(2)]
        back = [psum.tile([P, P], F32, name=f"back{h}", tag=("bank1_3", "bank1_1")[h]) for h in range(2)]

        for d in range(D):
            fetch_weighted(weighted[d][:], 0, d, P, V)
        for d in range(2):
            fetch_plain(d, 0, P)
        nc.tensor.transpose(turned[0][:], plain[0][:], ident[:])
        for d in range(D):
            nc.tensor.matmul(turned[D][:], weighted[d][:], ident[:], start=(d == 0), stop=(d == D - 1), is_transpose=True)
        fetch_plain(2, 0, P)
        nc.tensor.transpose(turned[1][:], plain[1][:], ident[:])
        nc.tensor.transpose(turned[2][:], plain[2][:], ident[:])
        for e in (0, D, 1, 2):
            if e == D:
                nc.scalar.copy(turned_sb[e], turned[e][:])
                nc.tensor.transpose(back[1][:], turned_sb[e], ident[:])
            else:
                nc.scalar.activation(turned_sb[e], turned[e][:], ACT.Copy, scale=columns[:, e:e + 1])
                nc.tensor.matmul(back[0][:], turned_sb[e], ident[:], start=(e == 0), stop=(e == 2), is_transpose=True)
        for h in (1, 0):
            nc.scalar.copy(res[0][:, halves[h]], back[h][:])
            (nc.scalar, nc.sync)[h].dma_start(out[0:P, halves[h]], res[0][:, halves[h]])

        fetch_weighted(terms[:, 0, 0:V], 1, 0, 0, V)
        fetch_weighted(terms[:, 1, 0:V], 1, 1, 0, V)
        fetch_weighted(terms[:, 2, 0:192], 1, 2, 0, 192)
        nc.vector.tensor_tensor(part[:], terms[:, 0, :], terms[:, 1, :], ALU.add)
        fetch_weighted(terms[:, 2, 192:V], 1, 2, 192, V)
        for lo, hi in ((0, 192), (192, V)):
            nc.vector.tensor_tensor(res[1][:, lo:hi], part[:, lo:hi], terms[:, 2, lo:hi], ALU.add)
            nc.sync.dma_start(out[P:N, lo:hi], res[1][:, lo:hi])
